import numpy as np
import ml_dtypes


def mxq(x, axis, fmt="e4m3"):
    dtype, down = {"e4m3": (ml_dtypes.float8_e4m3fn, 7), "e5m2": (ml_dtypes.float8_e5m2, 14)}[fmt]
    v = np.moveaxis(np.asarray(x, np.float32).astype(ml_dtypes.bfloat16).astype(np.float64), axis, -1)
    blocks = v.reshape(v.shape[:-1] + (-1, 32))
    amax = np.abs(blocks).max(-1, keepdims=True)
    byte = np.maximum(np.where(amax > 0, np.frexp(amax)[1] - 1 + 127, 0) - down, 1)
    scale = np.exp2(byte - 127.0)
    codes = (blocks / scale).astype(np.float32).astype(dtype).astype(np.float64)
    return np.moveaxis((codes * scale).reshape(v.shape), -1, axis)


WIDE = False


def mx_kscale(k):
    if not WIDE:
        return np.ones(k)
    levels = np.array([10, -10, 5, -5, 0])
    if k % 512:
        return np.exp2(np.random.permutation(np.resize(levels, k // 32))).repeat(32)
    a = np.empty((k // 512, 16))
    for p in range(k // 512):
        a[p, :8] = np.random.permutation(np.resize(levels, 8))
        for g in range(8):
            far = levels[np.abs(levels - a[p, g]) >= 10]
            a[p, g + 8] = far[np.random.randint(len(far))]
    return np.exp2(a.ravel()).repeat(32)


def f64(x):
    return np.asarray(x).astype(np.float64)


def split(x):
    m, e = np.frexp(f64(x))
    hi = np.ldexp(np.trunc(16.0 * m) / 16.0, e)
    return hi, f64(x) - hi


K, M, T = 512, 1536, 512


def setup_inputs():
    n = np.random.standard_normal
    s = mx_kscale(K)[:, None]
    return {
        "w": (n((K, M)) / np.sqrt(K) / s).astype(np.float32),
        "x": (n((K, T)) * s).astype(np.float32),
        "g": (n((1536, 512))).astype(np.float32),
    }


def reference(w, x, g):
    w_hi, w_lo = split(w)
    w_hi_, w_lo_ = mxq(w_hi, 0, "e4m3"), mxq(w_lo, 0, "e4m3")
    x_hi, x_lo = split(x)
    x_hi_, x_lo_ = mxq(x_hi, 0, "e4m3"), mxq(x_lo, 0, "e4m3")
    y = w_hi_.T @ x_hi_ + w_hi_.T @ x_lo_ + w_lo_.T @ x_hi_
    return f64(g) * y

@@ -1,0 +1,152 @@
+from contextlib import ExitStack
+
+import concourse.mybir as mybir
+
+K, M, T = 512, 1536, 512
+FLOPS = 3 * 2 * K * M * T
+
+F32 = mybir.dt.float32
+BF16 = mybir.dt.bfloat16
+I32 = mybir.dt.int32
+U32 = mybir.dt.uint32
+U8 = mybir.dt.uint8
+FP8X4 = mybir.dt.float8_e4m3fn_x4
+ALU = mybir.AluOpType
+
+P = 128
+PACK = 4
+RUN = 2
+PAIR_MASK = 0xFFF0FFF0 - (1 << 32)
+CHUNK = 256
+N_CHUNKS = M // CHUNK
+TILES_PER_CHUNK = CHUNK // P
+X_PIECES = [64, 64, 128, 128, 128]
+LOADS = [("w", 0, 1), ("w", 1, 1), ("w", 2, 1), ("g", 0, 1), ("w", 3, 1), ("g", 1, 2), ("w", 4, 2), ("g", 3, 3)]
+LAG = 2
+
+
+def tile_mix_split3_fm_mul_kernel(tc, w, x, g, out):
+    nc = tc.nc
+    with ExitStack() as ctx:
+        sb = ctx.enter_context(tc.tile_pool(name="sb", bufs=1))
+        psum = ctx.enter_context(tc.psum_pool(name="psum", bufs=8))
+        ctx.enter_context(tc.manual_schedule())
+
+        warm_in = sb.tile([P, 2], BF16, name="warm_in")
+        warm_out = sb.tile([P, 2], BF16, name="warm_out")
+        nc.vector.memset(warm_in[:], 0.0)
+        nc.scalar.copy(out=warm_out[:], in_=warm_in[:])
+
+        x_rows = x.rearrange("(p j) t -> p j t", j=PACK)
+        w_rows = w.rearrange("(p j) n -> p j n", j=PACK)
+        g_rows = g.rearrange("(a p) t -> p a t", p=P)
+        out_rows = out.rearrange("(a p) t -> p a t", p=P)
+
+        x_codes = [sb.tile([P, T], U32, name=f"x_codes{h}", align_bytes=64) for h in range(2)]
+        x_scales = [sb.tile([P, T], U8, name=f"x_scales{h}", align_bytes=64) for h in range(2)]
+        w_codes = [[sb.tile([P, CHUNK], U32, name=f"w_codes{c}_{h}", align_bytes=64) for h in range(2)] for c in range(N_CHUNKS)]
+        w_scales = [[sb.tile([P, CHUNK], U8, name=f"w_scales{c}_{h}", align_bytes=64) for h in range(2)] for c in range(N_CHUNKS)]
+
+        pieces = []
+        col = 0
+        for i, width in enumerate(X_PIECES):
+            raw = sb.tile([P, PACK, width], F32, name=f"x_raw{i}", align_bytes=64)
+            nc.sync.dma_start(out=raw[:], in_=x_rows[:, :, col : col + width])
+            cols = slice(col, col + width)
+            pieces.append((raw, 0, width, [t[:, cols] for t in x_codes], [t[:, cols] for t in x_scales]))
+            col += width
+        g_tiles = {}
+        w_pieces = {}
+        for kind, first, count in LOADS:
+            if kind == "w":
+                raw = sb.tile([P, PACK, count * CHUNK], F32, name=f"w_raw{first}", align_bytes=64)
+                nc.sync.dma_start(out=raw[:], in_=w_rows[:, :, first * CHUNK : (first + count) * CHUNK])
+                for c in range(count):
+                    w_pieces[first + c] = (raw, c * CHUNK, CHUNK, [t[:] for t in w_codes[first + c]], [t[:] for t in w_scales[first + c]])
+            else:
+                a0, na = first * TILES_PER_CHUNK, count * TILES_PER_CHUNK
+                g_sb = sb.tile([P, na, T], F32, name=f"g_sb{first}", align_bytes=64)
+                nc.sync.dma_start(out=g_sb[:], in_=g_rows[:, a0 : a0 + na, :])
+                for a in range(na):
+                    g_tiles[a0 + a] = g_sb[:, a, :]
+        pieces.extend(w_pieces[c] for c in range(N_CHUNKS))
+
+        hi = [sb.tile([P, p[2] * PACK], BF16, name=f"hi{i}", align_bytes=64) for i, p in enumerate(pieces)]
+        lo = [sb.tile([P, p[2] * PACK], BF16, name=f"lo{i}", align_bytes=64) for i, p in enumerate(pieces)]
+
+        def interleaved(t):
+            return t[:].rearrange("p (c i j) -> p c j i", i=RUN, j=PACK)
+
+        def truncate(i):
+            raw, c0, width = pieces[i][:3]
+            halves = raw[:].bitcast(BF16).rearrange("p j (c i h) -> p c j i h", i=RUN, h=2)
+            nc.scalar.copy(out=interleaved(hi[i]), in_=halves[:, c0 // RUN : (c0 + width) // RUN, :, :, 1])
+
+        def mask(i):
+            words = hi[i][:].bitcast(I32)
+            nc.vector.tensor_scalar(out=words, in0=words, scalar1=PAIR_MASK, scalar2=None, op0=ALU.bitwise_and)
+
+        def subtract(i):
+            raw, c0, width = pieces[i][:3]
+            src = raw[:].rearrange("p j (c i) -> p c j i", i=RUN)[:, c0 // RUN : (c0 + width) // RUN, :, :]
+            nc.vector.tensor_tensor(out=interleaved(lo[i]), in0=src, in1=interleaved(hi[i]), op=ALU.subtract)
+
+        def quantize(i, h):
+            nc.vector.quantize_mx(out=pieces[i][3][h].bitcast(FP8X4), scales=pieces[i][4][h], in_=(hi, lo)[h][i][:])
+
+        acc = {}
+
+        def multiply(a, wh, xh, start, stop):
+            c, cols = a // TILES_PER_CHUNK, slice((a % TILES_PER_CHUNK) * P, (a % TILES_PER_CHUNK + 1) * P)
+            nc.tensor.matmul_mx(
+                out=acc[a][:],
+                lhsT=w_codes[c][wh][:, cols].bitcast(FP8X4),
+                lhsT_scale=w_scales[c][wh][:, cols],
+                rhs=x_codes[xh][:].bitcast(FP8X4),
+                rhs_scale=x_scales[xh][:],
+                start=start,
+                stop=stop,
+            )
+
+        def tiles_of(c):
+            return range(c * TILES_PER_CHUNK, (c + 1) * TILES_PER_CHUNK)
+
+        def hi_products(c):
+            for a in tiles_of(c):
+                acc[a] = psum.tile([P, T], F32, name="acc")
+                multiply(a, 0, 0, True, False)
+                multiply(a, 0, 1, False, False)
+
+        def lo_products(c):
+            for a in tiles_of(c):
+                multiply(a, 1, 0, False, True)
+
+        def epilogue(c):
+            res = sb.tile([P, TILES_PER_CHUNK, T], F32, name=f"res{c}", align_bytes=64)
+            a0 = c * TILES_PER_CHUNK
+            for a in tiles_of(c):
+                nc.vector.tensor_tensor(out=res[:, a - a0, :], in0=acc[a][:], in1=g_tiles[a], op=ALU.mult)
+                if c == N_CHUNKS - 1:
+                    nc.sync.dma_start(out=out_rows[:, a, :], in_=res[:, a - a0, :])
+            if c < N_CHUNKS - 1:
+                nc.sync.dma_start(out=out_rows[:, a0 : a0 + TILES_PER_CHUNK, :], in_=res[:])
+
+        nx = len(X_PIECES)
+        for i in range(len(pieces)):
+            c = i - nx
+            truncate(i)
+            mask(i)
+            if i > 0:
+                quantize(i - 1, 1)
+            if c >= 1:
+                lo_products(c - 1)
+            if c >= LAG:
+                epilogue(c - LAG)
+            subtract(i)
+            quantize(i, 0)
+            if c >= 0:
+                hi_products(c)
+        quantize(len(pieces) - 1, 1)
+        lo_products(N_CHUNKS - 1)
+        for c in range(N_CHUNKS - LAG, N_CHUNKS):
+            epilogue(c)

@@ -17,12 +17,13 @@ P = 128
 PACK = 4
 RUN = 2
 PAIR_MASK = 0xFFF0FFF0 - (1 << 32)
-CHUNK = 256
-N_CHUNKS = M // CHUNK
-TILES_PER_CHUNK = CHUNK // P
-X_PIECES = [64, 64, 128, 128, 128]
-LOADS = [("w", 0, 1), ("w", 1, 1), ("w", 2, 1), ("g", 0, 1), ("w", 3, 1), ("g", 1, 2), ("w", 4, 2), ("g", 3, 3)]
+X_PIECES = [64,64,128,128,128]
+CHUNK_TILES = [2,2,2,2,2,1,1]
+N_CHUNKS = len(CHUNK_TILES)
+FIRST_TILE = [sum(CHUNK_TILES[:c]) for c in range(N_CHUNKS + 1)]
+LOADS = [["w",0,2],["w",2,2],["w",4,2],["g",0,2],["w",6,2],["g",2,2],["w",8,2],["g",4,2],["w",10,2],["g",6,6]]
 LAG = 2
+GPSIMD_COLS = [0,0,112,112,112,128,128]
 
 
 def tile_mix_split3_fm_mul_kernel(tc, w, x, g, out):
@@ -42,111 +43,119 @@ def tile_mix_split3_fm_mul_kernel(tc, w, x, g, out):
         g_rows = g.rearrange("(a p) t -> p a t", p=P)
         out_rows = out.rearrange("(a p) t -> p a t", p=P)
 
-        x_codes = [sb.tile([P, T], U32, name=f"x_codes{h}", align_bytes=64) for h in range(2)]
-        x_scales = [sb.tile([P, T], U8, name=f"x_scales{h}", align_bytes=64) for h in range(2)]
-        w_codes = [[sb.tile([P, CHUNK], U32, name=f"w_codes{c}_{h}", align_bytes=64) for h in range(2)] for c in range(N_CHUNKS)]
-        w_scales = [[sb.tile([P, CHUNK], U8, name=f"w_scales{c}_{h}", align_bytes=64) for h in range(2)] for c in range(N_CHUNKS)]
-
-        pieces = []
+        raw = []
         col = 0
         for i, width in enumerate(X_PIECES):
-            raw = sb.tile([P, PACK, width], F32, name=f"x_raw{i}", align_bytes=64)
-            nc.sync.dma_start(out=raw[:], in_=x_rows[:, :, col : col + width])
-            cols = slice(col, col + width)
-            pieces.append((raw, 0, width, [t[:, cols] for t in x_codes], [t[:, cols] for t in x_scales]))
+            stage = sb.tile([P, PACK, width], F32, name=f"x_raw{i}", align_bytes=64)
+            nc.sync.dma_start(out=stage[:], in_=x_rows[:, :, col : col + width])
+            raw.append((stage, 0, width))
             col += width
         g_tiles = {}
-        w_pieces = {}
-        for kind, first, count in LOADS:
+        w_stage = {}
+        for kind, a0, na in LOADS:
             if kind == "w":
-                raw = sb.tile([P, PACK, count * CHUNK], F32, name=f"w_raw{first}", align_bytes=64)
-                nc.sync.dma_start(out=raw[:], in_=w_rows[:, :, first * CHUNK : (first + count) * CHUNK])
-                for c in range(count):
-                    w_pieces[first + c] = (raw, c * CHUNK, CHUNK, [t[:] for t in w_codes[first + c]], [t[:] for t in w_scales[first + c]])
-            else:
-                a0, na = first * TILES_PER_CHUNK, count * TILES_PER_CHUNK
-                g_sb = sb.tile([P, na, T], F32, name=f"g_sb{first}", align_bytes=64)
-                nc.sync.dma_start(out=g_sb[:], in_=g_rows[:, a0 : a0 + na, :])
+                stage = sb.tile([P, PACK, na * P], F32, name=f"w_raw{a0}", align_bytes=64)
+                nc.sync.dma_start(out=stage[:], in_=w_rows[:, :, a0 * P : (a0 + na) * P])
                 for a in range(na):
-                    g_tiles[a0 + a] = g_sb[:, a, :]
-        pieces.extend(w_pieces[c] for c in range(N_CHUNKS))
+                    w_stage[a0 + a] = (stage, a * P)
+            else:
+                stage = sb.tile([P, na, T], F32, name=f"g_sb{a0}", align_bytes=64)
+                nc.sync.dma_start(out=stage[:], in_=g_rows[:, a0 : a0 + na, :])
+                for a in range(na):
+                    g_tiles[a0 + a] = stage[:, a, :]
+        for c in range(N_CHUNKS):
+            raw.append(w_stage[FIRST_TILE[c]] + (CHUNK_TILES[c] * P,))
 
-        hi = [sb.tile([P, p[2] * PACK], BF16, name=f"hi{i}", align_bytes=64) for i, p in enumerate(pieces)]
-        lo = [sb.tile([P, p[2] * PACK], BF16, name=f"lo{i}", align_bytes=64) for i, p in enumerate(pieces)]
+        parts = [sb.tile([P, 2, r[2] * PACK], BF16, name=f"parts{i}", align_bytes=64) for i, r in enumerate(raw)]
+        x_codes = sb.tile([P, 2, T], U32, name="x_codes", align_bytes=64)
+        x_scales = sb.tile([P, 2, T], U8, name="x_scales", align_bytes=64)
+        w_codes = [sb.tile([P, 2, n * P], U32, name=f"w_codes{c}", align_bytes=64) for c, n in enumerate(CHUNK_TILES)]
+        w_scales = [sb.tile([P, 2, n * P], U8, name=f"w_scales{c}", align_bytes=64) for c, n in enumerate(CHUNK_TILES)]
+        nx = len(X_PIECES)
 
-        def interleaved(t):
-            return t[:].rearrange("p (c i j) -> p c j i", i=RUN, j=PACK)
+        def part(i, h, c0, c1, run):
+            return parts[i][:, h, c0 * PACK : c1 * PACK].rearrange("p (c i j) -> p c j i", i=run, j=PACK)
 
         def truncate(i):
-            raw, c0, width = pieces[i][:3]
-            halves = raw[:].bitcast(BF16).rearrange("p j (c i h) -> p c j i h", i=RUN, h=2)
-            nc.scalar.copy(out=interleaved(hi[i]), in_=halves[:, c0 // RUN : (c0 + width) // RUN, :, :, 1])
+            stage, first, width = raw[i]
+            halves = stage[:].bitcast(BF16).rearrange("p j (c i h) -> p c j i h", i=RUN, h=2)
+            nc.scalar.copy(out=part(i, 0, 0, width, RUN), in_=halves[:, first // RUN : (first + width) // RUN, :, :, 1])
 
         def mask(i):
-            words = hi[i][:].bitcast(I32)
+            words = parts[i][:, 0, :].bitcast(I32)
             nc.vector.tensor_scalar(out=words, in0=words, scalar1=PAIR_MASK, scalar2=None, op0=ALU.bitwise_and)
 
-        def subtract(i):
-            raw, c0, width = pieces[i][:3]
-            src = raw[:].rearrange("p j (c i) -> p c j i", i=RUN)[:, c0 // RUN : (c0 + width) // RUN, :, :]
-            nc.vector.tensor_tensor(out=interleaved(lo[i]), in0=src, in1=interleaved(hi[i]), op=ALU.subtract)
+        def subtract(engine, i, c0, c1, run):
+            stage, first = raw[i][:2]
+            src = stage[:, :, first + c0 : first + c1].rearrange("p j (c i) -> p c j i", i=run)
+            engine.tensor_tensor(out=part(i, 1, c0, c1, run), in0=src, in1=part(i, 0, c0, c1, run), op=ALU.subtract)
 
-        def quantize(i, h):
-            nc.vector.quantize_mx(out=pieces[i][3][h].bitcast(FP8X4), scales=pieces[i][4][h], in_=(hi, lo)[h][i][:])
+        def quantize_x(i, h):
+            cols = slice(sum(X_PIECES[:i]), sum(X_PIECES[: i + 1]))
+            nc.vector.quantize_mx(out=x_codes[:, h, cols].bitcast(FP8X4), scales=x_scales[:, h, cols], in_=parts[i][:, h, :])
+
+        def quantize_w_part(c, h):
+            nc.vector.quantize_mx(out=w_codes[c][:, h, :].bitcast(FP8X4), scales=w_scales[c][:, h, :], in_=parts[nx + c][:, h, :])
+
+        def quantize_w(c):
+            flat = "p h n -> p (h n)"
+            nc.vector.quantize_mx(
+                out=w_codes[c][:].rearrange(flat).bitcast(FP8X4),
+                scales=w_scales[c][:].rearrange(flat),
+                in_=parts[nx + c][:].rearrange(flat),
+            )
 
         acc = {}
 
-        def multiply(a, wh, xh, start, stop):
-            c, cols = a // TILES_PER_CHUNK, slice((a % TILES_PER_CHUNK) * P, (a % TILES_PER_CHUNK + 1) * P)
-            nc.tensor.matmul_mx(
-                out=acc[a][:],
-                lhsT=w_codes[c][wh][:, cols].bitcast(FP8X4),
-                lhsT_scale=w_scales[c][wh][:, cols],
-                rhs=x_codes[xh][:].bitcast(FP8X4),
-                rhs_scale=x_scales[xh][:],
-                start=start,
-                stop=stop,
-            )
-
-        def tiles_of(c):
-            return range(c * TILES_PER_CHUNK, (c + 1) * TILES_PER_CHUNK)
-
-        def hi_products(c):
-            for a in tiles_of(c):
-                acc[a] = psum.tile([P, T], F32, name="acc")
-                multiply(a, 0, 0, True, False)
-                multiply(a, 0, 1, False, False)
-
-        def lo_products(c):
-            for a in tiles_of(c):
-                multiply(a, 1, 0, False, True)
+        def products(c, pairs):
+            for a in range(FIRST_TILE[c], FIRST_TILE[c + 1]):
+                cols = slice((a - FIRST_TILE[c]) * P, (a - FIRST_TILE[c] + 1) * P)
+                for wh, xh in pairs:
+                    if (wh, xh) == (0, 0):
+                        acc[a] = psum.tile([P, T], F32, name="acc")
+                    nc.tensor.matmul_mx(
+                        out=acc[a][:],
+                        lhsT=w_codes[c][:, wh, cols].bitcast(FP8X4),
+                        lhsT_scale=w_scales[c][:, wh, cols],
+                        rhs=x_codes[:, xh, :].bitcast(FP8X4),
+                        rhs_scale=x_scales[:, xh, :],
+                        start=(wh, xh) == (0, 0),
+                        stop=(wh, xh) == (1, 0),
+                    )
 
         def epilogue(c):
-            res = sb.tile([P, TILES_PER_CHUNK, T], F32, name=f"res{c}", align_bytes=64)
-            a0 = c * TILES_PER_CHUNK
-            for a in tiles_of(c):
-                nc.vector.tensor_tensor(out=res[:, a - a0, :], in0=acc[a][:], in1=g_tiles[a], op=ALU.mult)
-                if c == N_CHUNKS - 1:
-                    nc.sync.dma_start(out=out_rows[:, a, :], in_=res[:, a - a0, :])
-            if c < N_CHUNKS - 1:
-                nc.sync.dma_start(out=out_rows[:, a0 : a0 + TILES_PER_CHUNK, :], in_=res[:])
+            a0, na = FIRST_TILE[c], CHUNK_TILES[c]
+            res = sb.tile([P, na, T], F32, name=f"res{c}", align_bytes=64)
+            for a in range(na):
+                nc.vector.tensor_tensor(out=res[:, a, :], in0=acc[a0 + a][:], in1=g_tiles[a0 + a], op=ALU.mult)
+            nc.sync.dma_start(out=out_rows[:, a0 : a0 + na, :], in_=res[:])
 
-        nx = len(X_PIECES)
-        for i in range(len(pieces)):
-            c = i - nx
+        for i in range(nx):
             truncate(i)
             mask(i)
             if i > 0:
-                quantize(i - 1, 1)
-            if c >= 1:
-                lo_products(c - 1)
+                quantize_x(i - 1, 1)
+            subtract(nc.vector, i, 0, X_PIECES[i], RUN)
+            quantize_x(i, 0)
+        for c in range(N_CHUNKS):
+            i, width, share = nx + c, CHUNK_TILES[c] * P, GPSIMD_COLS[c]
+            truncate(i)
+            mask(i)
+            if share > 0:
+                subtract(nc.gpsimd, i, 0, share, 1)
+            if c == 0:
+                quantize_x(nx - 1, 1)
+            else:
+                quantize_w(c - 1)
+                products(c - 1, [(0, 0), (0, 1), (1, 0)])
             if c >= LAG:
                 epilogue(c - LAG)
-            subtract(i)
-            quantize(i, 0)
-            if c >= 0:
-                hi_products(c)
-        quantize(len(pieces) - 1, 1)
-        lo_products(N_CHUNKS - 1)
+            if share < width:
+                subtract(nc.vector, i, share, width, RUN)
+        last = N_CHUNKS - 1
+        quantize_w_part(last, 0)
+        products(last, [(0, 0), (0, 1)])
+        quantize_w_part(last, 1)
+        products(last, [(1, 0)])
         for c in range(N_CHUNKS - LAG, N_CHUNKS):
             epilogue(c)

@@ -15,22 +15,35 @@ ALU = mybir.AluOpType
 
 P = 128
 PACK = 4
-RUN = 2
+HI, LO = 0, 1
+PSUM_BANKS = 8
+
+WORD_MASK = 0xFFF00000 - (1 << 32)
 PAIR_MASK = 0xFFF0FFF0 - (1 << 32)
-X_PIECES = [64,64,128,128,128]
-CHUNK_TILES = [2,2,2,2,2,1,1]
-N_CHUNKS = len(CHUNK_TILES)
-FIRST_TILE = [sum(CHUNK_TILES[:c]) for c in range(N_CHUNKS + 1)]
-LOADS = [["w",0,2],["w",2,2],["w",4,2],["g",0,2],["w",6,2],["g",2,2],["w",8,2],["g",4,2],["w",10,2],["g",6,6]]
+
+RUN = 2
+ROWS_IN_RUNS = "p j (c i) -> p c j i"
+SIDE_BY_SIDE_IN_RUNS = "p (c i j) -> p c j i"
+
+X_WIDTH = 128
+X_PIECES = T // X_WIDTH
+CHUNK_TILES = [2, 2, 2, 2, 2, 1, 1]
+CHUNKS = len(CHUNK_TILES)
+FIRST_TILE = [sum(CHUNK_TILES[:c]) for c in range(CHUNKS)]
 LAG = 2
-GPSIMD_COLS = [0,0,112,112,112,128,128]
+LOADS = [
+    ("w", 0, 2), ("w", 2, 2), ("w", 4, 2), ("g", 0, 2), ("w", 6, 2),
+    ("g", 2, 2), ("w", 8, 2), ("g", 4, 2), ("w", 10, 2), ("g", 6, 6),
+]
+HI_PRODUCTS = [(HI, HI), (HI, LO)]
+LO_PRODUCTS = [(LO, HI)]
 
 
 def tile_mix_split3_fm_mul_kernel(tc, w, x, g, out):
     nc = tc.nc
     with ExitStack() as ctx:
         sb = ctx.enter_context(tc.tile_pool(name="sb", bufs=1))
-        psum = ctx.enter_context(tc.psum_pool(name="psum", bufs=8))
+        psum = ctx.enter_context(tc.psum_pool(name="psum", bufs=PSUM_BANKS))
         ctx.enter_context(tc.manual_schedule())
 
         warm_in = sb.tile([P, 2], BF16, name="warm_in")
@@ -40,122 +53,161 @@ def tile_mix_split3_fm_mul_kernel(tc, w, x, g, out):
 
         x_rows = x.rearrange("(p j) t -> p j t", j=PACK)
         w_rows = w.rearrange("(p j) n -> p j n", j=PACK)
-        g_rows = g.rearrange("(a p) t -> p a t", p=P)
-        out_rows = out.rearrange("(a p) t -> p a t", p=P)
+        g_tiles = g.rearrange("(a p) t -> p a t", p=P)
+        out_tiles = out.rearrange("(a p) t -> p a t", p=P)
 
-        raw = []
-        col = 0
-        for i, width in enumerate(X_PIECES):
-            stage = sb.tile([P, PACK, width], F32, name=f"x_raw{i}", align_bytes=64)
-            nc.sync.dma_start(out=stage[:], in_=x_rows[:, :, col : col + width])
-            raw.append((stage, 0, width))
-            col += width
-        g_tiles = {}
-        w_stage = {}
-        for kind, a0, na in LOADS:
-            if kind == "w":
-                stage = sb.tile([P, PACK, na * P], F32, name=f"w_raw{a0}", align_bytes=64)
-                nc.sync.dma_start(out=stage[:], in_=w_rows[:, :, a0 * P : (a0 + na) * P])
-                for a in range(na):
-                    w_stage[a0 + a] = (stage, a * P)
+        source = []
+        for i in range(X_PIECES):
+            stage = sb.tile([P, PACK, X_WIDTH], F32, name=f"x_raw{i}", align_bytes=64)
+            nc.sync.dma_start(out=stage[:], in_=x_rows[:, :, i * X_WIDTH : (i + 1) * X_WIDTH])
+            source.append((stage, 0, X_WIDTH))
+        w_place = {}
+        g_sb = {}
+        for operand, first, count in LOADS:
+            if operand == "w":
+                stage = sb.tile([P, PACK, count * P], F32, name=f"w_raw{first}", align_bytes=64)
+                nc.sync.dma_start(out=stage[:], in_=w_rows[:, :, first * P : (first + count) * P])
+                for a in range(count):
+                    w_place[first + a] = (stage, a * P)
             else:
-                stage = sb.tile([P, na, T], F32, name=f"g_sb{a0}", align_bytes=64)
-                nc.sync.dma_start(out=stage[:], in_=g_rows[:, a0 : a0 + na, :])
-                for a in range(na):
-                    g_tiles[a0 + a] = stage[:, a, :]
-        for c in range(N_CHUNKS):
-            raw.append(w_stage[FIRST_TILE[c]] + (CHUNK_TILES[c] * P,))
+                stage = sb.tile([P, count, T], F32, name=f"g_sb{first}", align_bytes=64)
+                nc.sync.dma_start(out=stage[:], in_=g_tiles[:, first : first + count, :])
+                for a in range(count):
+                    g_sb[first + a] = stage[:, a, :]
+        for c in range(CHUNKS):
+            source.append(w_place[FIRST_TILE[c]] + (CHUNK_TILES[c] * P,))
 
-        parts = [sb.tile([P, 2, r[2] * PACK], BF16, name=f"parts{i}", align_bytes=64) for i, r in enumerate(raw)]
+        parts = [sb.tile([P, 2, s[2] * PACK], BF16, name=f"parts{i}", align_bytes=64) for i, s in enumerate(source)]
         x_codes = sb.tile([P, 2, T], U32, name="x_codes", align_bytes=64)
         x_scales = sb.tile([P, 2, T], U8, name="x_scales", align_bytes=64)
         w_codes = [sb.tile([P, 2, n * P], U32, name=f"w_codes{c}", align_bytes=64) for c, n in enumerate(CHUNK_TILES)]
         w_scales = [sb.tile([P, 2, n * P], U8, name=f"w_scales{c}", align_bytes=64) for c, n in enumerate(CHUNK_TILES)]
-        nx = len(X_PIECES)
+        sums = {}
 
-        def part(i, h, c0, c1, run):
-            return parts[i][:, h, c0 * PACK : c1 * PACK].rearrange("p (c i j) -> p c j i", i=run, j=PACK)
+        def raw_runs(i, c0, c1):
+            stage, first = source[i][:2]
+            return stage[:, :, first + c0 : first + c1].rearrange(ROWS_IN_RUNS, i=RUN)
+
+        def part_runs(i, h, c0, c1):
+            return parts[i][:, h, c0 * PACK : c1 * PACK].rearrange(SIDE_BY_SIDE_IN_RUNS, i=RUN, j=PACK)
 
         def truncate(i):
-            stage, first, width = raw[i]
+            stage, first, width = source[i]
             halves = stage[:].bitcast(BF16).rearrange("p j (c i h) -> p c j i h", i=RUN, h=2)
-            nc.scalar.copy(out=part(i, 0, 0, width, RUN), in_=halves[:, first // RUN : (first + width) // RUN, :, :, 1])
+            upper = halves[:, first // RUN : (first + width) // RUN, :, :, 1]
+            nc.scalar.copy(out=part_runs(i, HI, 0, width), in_=upper)
 
         def mask(i):
-            words = parts[i][:, 0, :].bitcast(I32)
+            words = parts[i][:, HI, :].bitcast(I32)
             nc.vector.tensor_scalar(out=words, in0=words, scalar1=PAIR_MASK, scalar2=None, op0=ALU.bitwise_and)
 
-        def subtract(engine, i, c0, c1, run):
-            stage, first = raw[i][:2]
-            src = stage[:, :, first + c0 : first + c1].rearrange("p j (c i) -> p c j i", i=run)
-            engine.tensor_tensor(out=part(i, 1, c0, c1, run), in0=src, in1=part(i, 0, c0, c1, run), op=ALU.subtract)
+        def subtract(i, c0, c1):
+            nc.vector.tensor_tensor(
+                out=part_runs(i, LO, c0, c1), in0=raw_runs(i, c0, c1), in1=part_runs(i, HI, c0, c1), op=ALU.subtract
+            )
+
+        def interleave_first_tile(i):
+            rows = sb.tile([P, P * PACK], F32, name=f"rows{i}", align_bytes=64)
+            nc.scalar.copy(out=rows[:].rearrange(SIDE_BY_SIDE_IN_RUNS, i=RUN, j=PACK), in_=raw_runs(i, 0, P))
+            return rows
+
+        def subtract_first_tile_on_gpsimd(i, rows):
+            cols = slice(0, P * PACK)
+            nc.gpsimd.tensor_tensor(out=parts[i][:, LO, cols], in0=rows[:], in1=parts[i][:, HI, cols], op=ALU.subtract)
 
         def quantize_x(i, h):
-            cols = slice(sum(X_PIECES[:i]), sum(X_PIECES[: i + 1]))
+            cols = slice(i * X_WIDTH, (i + 1) * X_WIDTH)
             nc.vector.quantize_mx(out=x_codes[:, h, cols].bitcast(FP8X4), scales=x_scales[:, h, cols], in_=parts[i][:, h, :])
 
-        def quantize_w_part(c, h):
-            nc.vector.quantize_mx(out=w_codes[c][:, h, :].bitcast(FP8X4), scales=w_scales[c][:, h, :], in_=parts[nx + c][:, h, :])
+        def quantize_w(c, h):
+            nc.vector.quantize_mx(
+                out=w_codes[c][:, h, :].bitcast(FP8X4), scales=w_scales[c][:, h, :], in_=parts[X_PIECES + c][:, h, :]
+            )
 
-        def quantize_w(c):
+        def quantize_w_both(c):
             flat = "p h n -> p (h n)"
             nc.vector.quantize_mx(
                 out=w_codes[c][:].rearrange(flat).bitcast(FP8X4),
                 scales=w_scales[c][:].rearrange(flat),
-                in_=parts[nx + c][:].rearrange(flat),
+                in_=parts[X_PIECES + c][:].rearrange(flat),
             )
 
-        acc = {}
-
-        def products(c, pairs):
-            for a in range(FIRST_TILE[c], FIRST_TILE[c + 1]):
-                cols = slice((a - FIRST_TILE[c]) * P, (a - FIRST_TILE[c] + 1) * P)
-                for wh, xh in pairs:
-                    if (wh, xh) == (0, 0):
-                        acc[a] = psum.tile([P, T], F32, name="acc")
+        def multiply(c, products):
+            for a in range(CHUNK_TILES[c]):
+                tile_id, cols = FIRST_TILE[c] + a, slice(a * P, (a + 1) * P)
+                for w_part, x_part in products:
+                    opens = (w_part, x_part) == HI_PRODUCTS[0]
+                    if opens:
+                        sums[tile_id] = psum.tile([P, T], F32, name="sums")
                     nc.tensor.matmul_mx(
-                        out=acc[a][:],
-                        lhsT=w_codes[c][:, wh, cols].bitcast(FP8X4),
-                        lhsT_scale=w_scales[c][:, wh, cols],
-                        rhs=x_codes[:, xh, :].bitcast(FP8X4),
-                        rhs_scale=x_scales[:, xh, :],
-                        start=(wh, xh) == (0, 0),
-                        stop=(wh, xh) == (1, 0),
+                        out=sums[tile_id][:],
+                        lhsT=w_codes[c][:, w_part, cols].bitcast(FP8X4),
+                        lhsT_scale=w_scales[c][:, w_part, cols],
+                        rhs=x_codes[:, x_part, :].bitcast(FP8X4),
+                        rhs_scale=x_scales[:, x_part, :],
+                        start=opens,
+                        stop=(w_part, x_part) == LO_PRODUCTS[-1],
                     )
 
-        def epilogue(c):
-            a0, na = FIRST_TILE[c], CHUNK_TILES[c]
-            res = sb.tile([P, na, T], F32, name=f"res{c}", align_bytes=64)
-            for a in range(na):
-                nc.vector.tensor_tensor(out=res[:, a, :], in0=acc[a0 + a][:], in1=g_tiles[a0 + a], op=ALU.mult)
-            nc.sync.dma_start(out=out_rows[:, a0 : a0 + na, :], in_=res[:])
+        def read_out(c):
+            first, count = FIRST_TILE[c], CHUNK_TILES[c]
+            result = sb.tile([P, count, T], F32, name=f"result{c}", align_bytes=64)
+            for a in range(count):
+                nc.vector.tensor_tensor(out=result[:, a, :], in0=sums[first + a][:], in1=g_sb[first + a], op=ALU.mult)
+            nc.sync.dma_start(out=out_tiles[:, first : first + count, :], in_=result[:])
 
-        for i in range(nx):
+        first_hi = sb.tile([P, PACK, X_WIDTH], F32, name="first_hi", align_bytes=64)
+        nc.vector.tensor_scalar(
+            out=first_hi[:].bitcast(I32),
+            in0=source[0][0][:].bitcast(I32),
+            scalar1=WORD_MASK,
+            scalar2=None,
+            op0=ALU.bitwise_and,
+        )
+        first_hi_runs = first_hi[:].rearrange(ROWS_IN_RUNS, i=RUN)
+        nc.vector.tensor_tensor(
+            out=part_runs(0, LO, 0, X_WIDTH), in0=raw_runs(0, 0, X_WIDTH), in1=first_hi_runs, op=ALU.subtract
+        )
+        for i in range(1, X_PIECES):
             truncate(i)
             mask(i)
-            if i > 0:
-                quantize_x(i - 1, 1)
-            subtract(nc.vector, i, 0, X_PIECES[i], RUN)
-            quantize_x(i, 0)
-        for c in range(N_CHUNKS):
-            i, width, share = nx + c, CHUNK_TILES[c] * P, GPSIMD_COLS[c]
+            if i > 1:
+                quantize_x(i - 1, HI)
+            quantize_x(i - 1, LO)
+            subtract(i, 0, X_WIDTH)
+        nc.scalar.copy(out=part_runs(0, HI, 0, X_WIDTH), in_=first_hi_runs)
+
+        for c in range(CHUNKS):
+            i, width = X_PIECES + c, CHUNK_TILES[c] * P
+            reads_out = c >= LAG
+            if reads_out:
+                rows = interleave_first_tile(i)
             truncate(i)
             mask(i)
-            if share > 0:
-                subtract(nc.gpsimd, i, 0, share, 1)
+            if reads_out:
+                subtract_first_tile_on_gpsimd(i, rows)
             if c == 0:
-                quantize_x(nx - 1, 1)
+                quantize_x(X_PIECES - 1, HI)
+                quantize_x(X_PIECES - 1, LO)
+                quantize_x(0, HI)
+                quantize_w(0, HI)
+                multiply(0, HI_PRODUCTS)
+            elif c == 1:
+                quantize_w(0, LO)
+                multiply(0, LO_PRODUCTS)
             else:
-                quantize_w(c - 1)
-                products(c - 1, [(0, 0), (0, 1), (1, 0)])
-            if c >= LAG:
-                epilogue(c - LAG)
-            if share < width:
-                subtract(nc.vector, i, share, width, RUN)
-        last = N_CHUNKS - 1
-        quantize_w_part(last, 0)
-        products(last, [(0, 0), (0, 1)])
-        quantize_w_part(last, 1)
-        products(last, [(1, 0)])
-        for c in range(N_CHUNKS - LAG, N_CHUNKS):
-            epilogue(c)
+                quantize_w_both(c - 1)
+                multiply(c - 1, HI_PRODUCTS + LO_PRODUCTS)
+            if reads_out:
+                read_out(c - LAG)
+            vector_from = P if reads_out else 0
+            if vector_from < width:
+                subtract(i, vector_from, width)
+
+        last = CHUNKS - 1
+        quantize_w(last, HI)
+        multiply(last, HI_PRODUCTS)
+        quantize_w(last, LO)
+        multiply(last, LO_PRODUCTS)
+        for c in range(CHUNKS - LAG, CHUNKS):
+            read_out(c)

@@ -1,6 +1,7 @@
 from contextlib import ExitStack
 
 import concourse.mybir as mybir
+from concourse.masks import make_identity
 
 K, M, T = 512, 1536, 512
 FLOPS = 3 * 2 * K * M * T
@@ -12,11 +13,13 @@ U32 = mybir.dt.uint32
 U8 = mybir.dt.uint8
 FP8X4 = mybir.dt.float8_e4m3fn_x4
 ALU = mybir.AluOpType
+ACT = mybir.ActivationFunctionType
 
 P = 128
 PACK = 4
 HI, LO = 0, 1
-PSUM_BANKS = 8
+SUM_BANKS = 5
+SIGN_BIT = -(1 << 31)
 
 WORD_MASK = 0xFFF00000 - (1 << 32)
 PAIR_MASK = 0xFFF0FFF0 - (1 << 32)
@@ -27,13 +30,12 @@ SIDE_BY_SIDE_IN_RUNS = "p (c i j) -> p c j i"
 
 X_WIDTH = 128
 X_PIECES = T // X_WIDTH
-CHUNK_TILES = [2, 2, 2, 2, 2, 1, 1]
-CHUNKS = len(CHUNK_TILES)
-FIRST_TILE = [sum(CHUNK_TILES[:c]) for c in range(CHUNKS)]
-LAG = 2
+TURNED_BANKS = 2
+CHUNKS = [[0, 1], [2, 3], [4, 5], [6, 7], [8, 9], [10], [11]]
+TENSOR_CHUNKS = [3, 4]
 LOADS = [
-    ("w", 0, 2), ("w", 2, 2), ("w", 4, 2), ("g", 0, 2), ("w", 6, 2),
-    ("g", 2, 2), ("w", 8, 2), ("g", 4, 2), ("w", 10, 2), ("g", 6, 6),
+    ("w", [0, 1]), ("w", [2, 3]), ("w", [4, 5]), ("w", [6, 7]), ("w", [8, 9]), ("g", [0, 1]),
+    ("g", [2, 3]), ("w", [10, 11]), ("g", [4, 5]), ("g", [6, 7]), ("g", [8, 9, 10, 11]),
 ]
 HI_PRODUCTS = [(HI, HI), (HI, LO)]
 LO_PRODUCTS = [(LO, HI)]
@@ -43,7 +45,9 @@ def tile_mix_split3_fm_mul_kernel(tc, w, x, g, out):
     nc = tc.nc
     with ExitStack() as ctx:
         sb = ctx.enter_context(tc.tile_pool(name="sb", bufs=1))
-        psum = ctx.enter_context(tc.psum_pool(name="psum", bufs=PSUM_BANKS))
+        psum = ctx.enter_context(tc.psum_pool(name="psum", bufs=SUM_BANKS))
+        psum_turned = ctx.enter_context(tc.psum_pool(name="psum_turned", bufs=TURNED_BANKS))
+        psum_back = ctx.enter_context(tc.psum_pool(name="psum_back", bufs=1))
         ctx.enter_context(tc.manual_schedule())
 
         warm_in = sb.tile([P, 2], BF16, name="warm_in")
@@ -51,163 +55,297 @@ def tile_mix_split3_fm_mul_kernel(tc, w, x, g, out):
         nc.vector.memset(warm_in[:], 0.0)
         nc.scalar.copy(out=warm_out[:], in_=warm_in[:])
 
+        identity = sb.tile([P, P], F32, name="identity", align_bytes=64)
+        make_identity(nc, identity[:])
+
         x_rows = x.rearrange("(p j) t -> p j t", j=PACK)
         w_rows = w.rearrange("(p j) n -> p j n", j=PACK)
         g_tiles = g.rearrange("(a p) t -> p a t", p=P)
         out_tiles = out.rearrange("(a p) t -> p a t", p=P)
 
-        source = []
-        for i in range(X_PIECES):
+        def stepped(tiles):
+            step = tiles[1] - tiles[0] if len(tiles) > 1 else 1
+            return slice(tiles[0], tiles[-1] + 1, step)
+
+        half = X_WIDTH // 2
+        x_halves = []
+        for e in range(2):
+            stage = sb.tile([P, PACK, half], F32, name=f"x_half{e}", align_bytes=64)
+            nc.sync.dma_start(out=stage[:], in_=x_rows[:, :, e * half : (e + 1) * half])
+            x_halves.append(stage)
+        x_raw = [None]
+        for i in range(1, X_PIECES):
             stage = sb.tile([P, PACK, X_WIDTH], F32, name=f"x_raw{i}", align_bytes=64)
             nc.sync.dma_start(out=stage[:], in_=x_rows[:, :, i * X_WIDTH : (i + 1) * X_WIDTH])
-            source.append((stage, 0, X_WIDTH))
+            x_raw.append(stage)
         w_place = {}
         g_sb = {}
-        for operand, first, count in LOADS:
+        for operand, tiles in LOADS:
             if operand == "w":
-                stage = sb.tile([P, PACK, count * P], F32, name=f"w_raw{first}", align_bytes=64)
-                nc.sync.dma_start(out=stage[:], in_=w_rows[:, :, first * P : (first + count) * P])
-                for a in range(count):
-                    w_place[first + a] = (stage, a * P)
+                stage = sb.tile([P, PACK, len(tiles) * P], F32, name=f"w_raw{tiles[0]}", align_bytes=64)
+                nc.sync.dma_start(out=stage[:], in_=w_rows[:, :, tiles[0] * P : (tiles[-1] + 1) * P])
+                for a, t in enumerate(tiles):
+                    w_place[t] = (stage, a * P)
             else:
-                stage = sb.tile([P, count, T], F32, name=f"g_sb{first}", align_bytes=64)
-                nc.sync.dma_start(out=stage[:], in_=g_tiles[:, first : first + count, :])
-                for a in range(count):
-                    g_sb[first + a] = stage[:, a, :]
-        for c in range(CHUNKS):
-            source.append(w_place[FIRST_TILE[c]] + (CHUNK_TILES[c] * P,))
+                stage = sb.tile([P, len(tiles), T], F32, name=f"g_sb{tiles[0]}", align_bytes=64)
+                nc.sync.dma_start(out=stage[:], in_=g_tiles[:, stepped(tiles), :])
+                for a, t in enumerate(tiles):
+                    g_sb[t] = stage[:, a, :]
 
-        parts = [sb.tile([P, 2, s[2] * PACK], BF16, name=f"parts{i}", align_bytes=64) for i, s in enumerate(source)]
+        x_parts = [sb.tile([P, 2 * X_WIDTH * PACK], BF16, name=f"x_parts{i}", align_bytes=64) for i in range(X_PIECES)]
+        w_parts = [sb.tile([P, 2 * len(ts) * P * PACK], BF16, name=f"w_parts{c}", align_bytes=64) for c, ts in enumerate(CHUNKS)]
         x_codes = sb.tile([P, 2, T], U32, name="x_codes", align_bytes=64)
         x_scales = sb.tile([P, 2, T], U8, name="x_scales", align_bytes=64)
-        w_codes = [sb.tile([P, 2, n * P], U32, name=f"w_codes{c}", align_bytes=64) for c, n in enumerate(CHUNK_TILES)]
-        w_scales = [sb.tile([P, 2, n * P], U8, name=f"w_scales{c}", align_bytes=64) for c, n in enumerate(CHUNK_TILES)]
+        w_codes = [sb.tile([P, 2 * len(ts) * P], U32, name=f"w_codes{c}", align_bytes=64) for c, ts in enumerate(CHUNKS)]
+        w_scales = [sb.tile([P, 2 * len(ts) * P], U8, name=f"w_scales{c}", align_bytes=64) for c, ts in enumerate(CHUNKS)]
         sums = {}
 
-        def raw_runs(i, c0, c1):
-            stage, first = source[i][:2]
-            return stage[:, :, first + c0 : first + c1].rearrange(ROWS_IN_RUNS, i=RUN)
+        def x_span(i):
+            n = X_WIDTH * PACK
+            return (x_raw[i], 0, X_WIDTH, x_parts[i][:, 0:n], x_parts[i][:, n : 2 * n])
 
-        def part_runs(i, h, c0, c1):
-            return parts[i][:, h, c0 * PACK : c1 * PACK].rearrange(SIDE_BY_SIDE_IN_RUNS, i=RUN, j=PACK)
+        def w_span(c, a0, a1):
+            stage, first = w_place[CHUNKS[c][a0]]
+            n = P * PACK
+            if c in TENSOR_CHUNKS:
+                return (stage, first, P, w_parts[c][:, 2 * a0 * n : (2 * a0 + 1) * n], w_parts[c][:, (2 * a0 + 1) * n : (2 * a0 + 2) * n])
+            low = len(CHUNKS[c]) * n
+            return (stage, first, (a1 - a0) * P, w_parts[c][:, a0 * n : a1 * n], w_parts[c][:, low + a0 * n : low + a1 * n])
 
-        def truncate(i):
-            stage, first, width = source[i]
+        def raw(span):
+            return span[0][:, :, span[1] : span[1] + span[2]]
+
+        def rows_in_runs(rows):
+            return rows.rearrange(ROWS_IN_RUNS, i=RUN)
+
+        def in_runs(part):
+            return part.rearrange(SIDE_BY_SIDE_IN_RUNS, i=RUN, j=PACK)
+
+        def truncate(span):
+            stage, first, width = span[:3]
             halves = stage[:].bitcast(BF16).rearrange("p j (c i h) -> p c j i h", i=RUN, h=2)
-            upper = halves[:, first // RUN : (first + width) // RUN, :, :, 1]
-            nc.scalar.copy(out=part_runs(i, HI, 0, width), in_=upper)
+            nc.scalar.copy(out=in_runs(span[3]), in_=halves[:, first // RUN : (first + width) // RUN, :, :, 1])
 
-        def mask(i):
-            words = parts[i][:, HI, :].bitcast(I32)
+        def mask(span):
+            words = span[3].bitcast(I32)
             nc.vector.tensor_scalar(out=words, in0=words, scalar1=PAIR_MASK, scalar2=None, op0=ALU.bitwise_and)
 
-        def subtract(i, c0, c1):
-            nc.vector.tensor_tensor(
-                out=part_runs(i, LO, c0, c1), in0=raw_runs(i, c0, c1), in1=part_runs(i, HI, c0, c1), op=ALU.subtract
+        def subtract(span):
+            nc.vector.tensor_tensor(out=in_runs(span[4]), in0=rows_in_runs(raw(span)), in1=in_runs(span[3]), op=ALU.subtract)
+
+        def mask_words(name, rows):
+            words = sb.tile(list(rows.shape), F32, name=name, align_bytes=64)
+            nc.vector.tensor_scalar(
+                out=words[:].bitcast(I32), in0=rows.bitcast(I32), scalar1=WORD_MASK, scalar2=None, op0=ALU.bitwise_and
+            )
+            return words
+
+        def subtract_words(low, rows, words):
+            nc.vector.tensor_tensor(out=in_runs(low), in0=rows_in_runs(rows), in1=rows_in_runs(words[:]), op=ALU.subtract)
+
+        def high_from_words(high, words):
+            nc.scalar.copy(out=in_runs(high), in_=rows_in_runs(words[:]))
+
+        def slot(c, a, h):
+            return 2 * a + h if c in TENSOR_CHUNKS else h * len(CHUNKS[c]) + a
+
+        def quantize_slots(c, s0, s1):
+            nc.vector.quantize_mx(
+                out=w_codes[c][:, s0 * P : s1 * P].bitcast(FP8X4),
+                scales=w_scales[c][:, s0 * P : s1 * P],
+                in_=w_parts[c][:, s0 * P * PACK : s1 * P * PACK],
             )
 
-        def interleave_first_tile(i):
-            rows = sb.tile([P, P * PACK], F32, name=f"rows{i}", align_bytes=64)
-            nc.scalar.copy(out=rows[:].rearrange(SIDE_BY_SIDE_IN_RUNS, i=RUN, j=PACK), in_=raw_runs(i, 0, P))
-            return rows
+        def quantize_w_tile(c, a, h):
+            quantize_slots(c, slot(c, a, h), slot(c, a, h) + 1)
 
-        def subtract_first_tile_on_gpsimd(i, rows):
-            cols = slice(0, P * PACK)
-            nc.gpsimd.tensor_tensor(out=parts[i][:, LO, cols], in0=rows[:], in1=parts[i][:, HI, cols], op=ALU.subtract)
+        laid_out = {}
+
+        def lay_out(c):
+            laid_out[c] = sb.tile([P, P * PACK], F32, name=f"rows{c}", align_bytes=64)
+            nc.scalar.copy(out=in_runs(laid_out[c][:]), in_=rows_in_runs(raw(w_span(c, 0, 1))))
+
+        def subtract_on_gpsimd(c):
+            span = w_span(c, 0, 1)
+            nc.gpsimd.tensor_tensor(out=span[4], in0=laid_out[c][:], in1=span[3], op=ALU.subtract)
+
+        negated = {}
+        turned = {}
+
+        def mask_negated(chunks):
+            stage, first = w_place[CHUNKS[chunks[0]][1]]
+            width = len(chunks) * P
+            words = sb.tile([P, PACK, width], F32, name=f"negated{chunks[0]}", align_bytes=64)
+            nc.vector.tensor_scalar(
+                out=words[:].bitcast(I32),
+                in0=stage[:, :, first : first + width].bitcast(I32),
+                scalar1=WORD_MASK,
+                scalar2=SIGN_BIT,
+                op0=ALU.bitwise_and,
+                op1=ALU.bitwise_xor,
+            )
+            for a, c in enumerate(chunks):
+                negated[c] = words[:, :, a * P : (a + 1) * P]
+
+        def turn_raw(c):
+            turned[c] = psum_turned.tile([P, PACK, P], F32, name="turned")
+            rows = raw(w_span(c, 1, 2))
+            for j in range(PACK):
+                nc.tensor.matmul(turned[c][:, j, :], lhsT=rows[:, j, :], rhs=identity[:], is_transpose=True, start=j == 0, stop=False)
+
+        def turn_negated(c):
+            for j in range(PACK):
+                nc.tensor.matmul(
+                    turned[c][:, j, :], lhsT=negated[c][:, j, :], rhs=identity[:], is_transpose=True, start=False, stop=j == PACK - 1
+                )
+
+        def high_from_negated(c):
+            nc.scalar.activation(out=in_runs(w_span(c, 1, 2)[3]), in_=rows_in_runs(negated[c]), func=ACT.Copy, scale=-1.0)
+
+        def round_turned(c):
+            pairs = sb.tile([P, PACK * P], BF16, name=f"pairs{c}", align_bytes=64)
+            nc.scalar.copy(
+                out=pairs[:].rearrange("n (u p e) -> n u p e", u=2, e=2),
+                in_=turned[c][:].rearrange("n (u e) p -> n u p e", e=2),
+            )
+            turned[c] = pairs
+
+        def turn_back(chunks):
+            bank = psum_back.tile([P, 2, 2, P], F32, name="back")
+            for a, c in enumerate(chunks):
+                words = turned[c][:].bitcast(F32)
+                for u in range(2):
+                    nc.tensor.transpose(bank[:, a, u, :], words[:, u * P : (u + 1) * P], identity[:])
+                turned[c] = bank[:, a, :, :]
+
+        def low_from_turned(c):
+            nc.scalar.copy(
+                out=w_span(c, 1, 2)[4].bitcast(F32).rearrange("p (n u) -> p n u", u=2),
+                in_=turned[c].rearrange("p u n -> p n u"),
+            )
 
         def quantize_x(i, h):
             cols = slice(i * X_WIDTH, (i + 1) * X_WIDTH)
-            nc.vector.quantize_mx(out=x_codes[:, h, cols].bitcast(FP8X4), scales=x_scales[:, h, cols], in_=parts[i][:, h, :])
+            nc.vector.quantize_mx(out=x_codes[:, h, cols].bitcast(FP8X4), scales=x_scales[:, h, cols], in_=x_span(i)[3 + h])
 
         def quantize_w(c, h):
-            nc.vector.quantize_mx(
-                out=w_codes[c][:, h, :].bitcast(FP8X4), scales=w_scales[c][:, h, :], in_=parts[X_PIECES + c][:, h, :]
-            )
+            quantize_slots(c, slot(c, 0, h), slot(c, 0, h) + len(CHUNKS[c]))
 
-        def quantize_w_both(c):
-            flat = "p h n -> p (h n)"
-            nc.vector.quantize_mx(
-                out=w_codes[c][:].rearrange(flat).bitcast(FP8X4),
-                scales=w_scales[c][:].rearrange(flat),
-                in_=parts[X_PIECES + c][:].rearrange(flat),
-            )
-
-        def multiply(c, products):
-            for a in range(CHUNK_TILES[c]):
-                tile_id, cols = FIRST_TILE[c] + a, slice(a * P, (a + 1) * P)
-                for w_part, x_part in products:
-                    opens = (w_part, x_part) == HI_PRODUCTS[0]
+        def multiply(c, products, t0=0, t1=T, only=None):
+            for a, t in enumerate(CHUNKS[c]):
+                for w_part, x_part in products if only in (None, a) else []:
+                    cols = slice(slot(c, a, w_part) * P, (slot(c, a, w_part) + 1) * P)
+                    opens = (w_part, x_part) == HI_PRODUCTS[0] and t0 == 0
                     if opens:
-                        sums[tile_id] = psum.tile([P, T], F32, name="sums")
+                        sums[t] = psum.tile([P, T], F32, name="sums")
                     nc.tensor.matmul_mx(
-                        out=sums[tile_id][:],
-                        lhsT=w_codes[c][:, w_part, cols].bitcast(FP8X4),
-                        lhsT_scale=w_scales[c][:, w_part, cols],
-                        rhs=x_codes[:, x_part, :].bitcast(FP8X4),
-                        rhs_scale=x_scales[:, x_part, :],
+                        out=sums[t][:, t0:t1],
+                        lhsT=w_codes[c][:, cols].bitcast(FP8X4),
+                        lhsT_scale=w_scales[c][:, cols],
+                        rhs=x_codes[:, x_part, t0:t1].bitcast(FP8X4),
+                        rhs_scale=x_scales[:, x_part, t0:t1],
                         start=opens,
-                        stop=(w_part, x_part) == LO_PRODUCTS[-1],
+                        stop=(w_part, x_part) == LO_PRODUCTS[-1] and t1 == T,
                     )
 
-        def read_out(c):
-            first, count = FIRST_TILE[c], CHUNK_TILES[c]
-            result = sb.tile([P, count, T], F32, name=f"result{c}", align_bytes=64)
-            for a in range(count):
-                nc.vector.tensor_tensor(out=result[:, a, :], in0=sums[first + a][:], in1=g_sb[first + a], op=ALU.mult)
-            nc.sync.dma_start(out=out_tiles[:, first : first + count, :], in_=result[:])
+        def read_out(tiles, t0=0, t1=T):
+            result = sb.tile([P, len(tiles), t1 - t0], F32, name=f"result{tiles[0]}_{t0}", align_bytes=64)
+            for t in tiles:
+                nc.vector.tensor_tensor(out=result[:, t - min(tiles), :], in0=sums[t][:, t0:t1], in1=g_sb[t][:, t0:t1], op=ALU.mult)
+            nc.sync.dma_start(out=out_tiles[:, min(tiles) : max(tiles) + 1, t0:t1], in_=result[:])
 
-        first_hi = sb.tile([P, PACK, X_WIDTH], F32, name="first_hi", align_bytes=64)
-        nc.vector.tensor_scalar(
-            out=first_hi[:].bitcast(I32),
-            in0=source[0][0][:].bitcast(I32),
-            scalar1=WORD_MASK,
-            scalar2=None,
-            op0=ALU.bitwise_and,
-        )
-        first_hi_runs = first_hi[:].rearrange(ROWS_IN_RUNS, i=RUN)
-        nc.vector.tensor_tensor(
-            out=part_runs(0, LO, 0, X_WIDTH), in0=raw_runs(0, 0, X_WIDTH), in1=first_hi_runs, op=ALU.subtract
-        )
-        for i in range(1, X_PIECES):
-            truncate(i)
-            mask(i)
-            if i > 1:
-                quantize_x(i - 1, HI)
-            quantize_x(i - 1, LO)
-            subtract(i, 0, X_WIDTH)
-        nc.scalar.copy(out=part_runs(0, HI, 0, X_WIDTH), in_=first_hi_runs)
+        n_half = half * PACK
+        high0, low0 = x_span(0)[3:]
+        words = [mask_words(f"x_words{e}", x_halves[e][:]) for e in range(2)]
+        for e in range(2):
+            high_from_words(high0[:, e * n_half : (e + 1) * n_half], words[e])
+            subtract_words(low0[:, e * n_half : (e + 1) * n_half], x_halves[e][:], words[e])
+        words1 = mask_words("x_words_1", x_raw[1][:])
+        truncate(x_span(2))
+        truncate(x_span(3))
+        high_from_words(x_span(1)[3], words1)
+        truncate(w_span(0, 0, 1))
+        truncate(w_span(0, 1, 2))
+        truncate(w_span(1, 0, 2))
+        quantize_x(0, HI)
+        quantize_x(0, LO)
+        subtract_words(x_span(1)[4], x_raw[1][:], words1)
+        mask(x_span(2))
+        quantize_x(1, LO)
+        subtract(x_span(2))
+        mask(x_span(3))
+        quantize_x(2, HI)
+        quantize_x(1, HI)
+        subtract(x_span(3))
+        mask(w_span(0, 0, 1))
+        quantize_x(2, LO)
+        quantize_x(3, HI)
+        quantize_w_tile(0, 0, HI)
+        mask(w_span(0, 1, 2))
+        quantize_x(3, LO)
+        multiply(0, HI_PRODUCTS, only=0)
+        quantize_w_tile(0, 1, HI)
+        multiply(0, HI_PRODUCTS, only=1)
+        subtract(w_span(0, 0, 2))
+        def masked(c):
+            return w_span(c, 0, 1 if c in TENSOR_CHUNKS else len(CHUNKS[c]))
 
-        for c in range(CHUNKS):
-            i, width = X_PIECES + c, CHUNK_TILES[c] * P
-            reads_out = c >= LAG
-            if reads_out:
-                rows = interleave_first_tile(i)
-            truncate(i)
-            mask(i)
-            if reads_out:
-                subtract_first_tile_on_gpsimd(i, rows)
-            if c == 0:
-                quantize_x(X_PIECES - 1, HI)
-                quantize_x(X_PIECES - 1, LO)
-                quantize_x(0, HI)
-                quantize_w(0, HI)
-                multiply(0, HI_PRODUCTS)
-            elif c == 1:
-                quantize_w(0, LO)
-                multiply(0, LO_PRODUCTS)
+        lay_out(2)
+        truncate(masked(2))
+        lay_out(3)
+        truncate(masked(3))
+        mask(masked(1))
+        mask_negated([3])
+        quantize_w(0, LO)
+        subtract(masked(1))
+        turn_raw(3)
+        turn_negated(3)
+        multiply(0, LO_PRODUCTS)
+        round_turned(3)
+        all_products = HI_PRODUCTS + LO_PRODUCTS
+        last = len(CHUNKS) - 1
+        order = [t for c, ts in enumerate(CHUNKS) for t in (ts[::-1] if c in TENSOR_CHUNKS else ts)]
+        done = 0
+        for c in range(2, last + 1):
+            if c + 2 in TENSOR_CHUNKS:
+                mask_negated([c + 2])
+            if c in TENSOR_CHUNKS:
+                turn_back([c])
+                low_from_turned(c)
+            if c + 1 in TENSOR_CHUNKS:
+                high_from_negated(c + 1)
+            if c + 2 <= last:
+                lay_out(c + 2)
+                truncate(masked(c + 2))
+            if c + 2 in TENSOR_CHUNKS:
+                turn_raw(c + 2)
+                turn_negated(c + 2)
+                round_turned(c + 2)
+            split_call = c - 1 in TENSOR_CHUNKS
+            if split_call:
+                quantize_slots(c - 1, 2, 4)
+                multiply(c - 1, all_products, only=1)
+            mask(masked(c))
+            subtract_on_gpsimd(c)
+            if split_call:
+                quantize_slots(c - 1, 0, 2)
+                multiply(c - 1, all_products, only=0)
             else:
-                quantize_w_both(c - 1)
-                multiply(c - 1, HI_PRODUCTS + LO_PRODUCTS)
-            if reads_out:
-                read_out(c - LAG)
-            vector_from = P if reads_out else 0
-            if vector_from < width:
-                subtract(i, vector_from, width)
-
-        last = CHUNKS - 1
-        quantize_w(last, HI)
-        multiply(last, HI_PRODUCTS)
+                quantize_slots(c - 1, 0, 2 * len(CHUNKS[c - 1]))
+                multiply(c - 1, all_products)
+            if c == last:
+                quantize_w(last, HI)
+                multiply(last, HI_PRODUCTS)
+            if c < last:
+                read_out(order[done : done + 2])
+            else:
+                read_out(order[done : done + 1])
+                read_out(order[done + 1 : done + 2])
+            done = done + 2
+            if len(CHUNKS[c]) > 1 and c not in TENSOR_CHUNKS:
+                subtract(w_span(c, 1, 2))
         quantize_w(last, LO)
         multiply(last, LO_PRODUCTS)
-        for c in range(CHUNKS - LAG, CHUNKS):
-            read_out(c)
+        read_out(CHUNKS[last - 1])
+        read_out(CHUNKS[last], 0, T // 2)
+        read_out(CHUNKS[last], T // 2, T)

@@ -31,11 +31,13 @@ SIDE_BY_SIDE_IN_RUNS = "p (c i j) -> p c j i"
 X_WIDTH = 128
 X_PIECES = T // X_WIDTH
 TURNED_BANKS = 2
+STORES = [[0, 1, 2, 3], [4, 5], [6, 7], [8, 9], [10], [11]]
+X_LOADS = [1, 1, 1, 1]
 CHUNKS = [[0, 1], [2, 3], [4, 5], [6, 7], [8, 9], [10], [11]]
 TENSOR_CHUNKS = [3, 4]
 LOADS = [
     ("w", [0, 1]), ("w", [2, 3]), ("w", [4, 5]), ("w", [6, 7]), ("w", [8, 9]), ("g", [0, 1]),
-    ("g", [2, 3]), ("w", [10, 11]), ("g", [4, 5]), ("g", [6, 7]), ("g", [8, 9, 10, 11]),
+    ("g", [2, 3, 4, 5]), ("w", [10, 11]), ("g", [6, 7, 8, 9, 10, 11]),
 ]
 HI_PRODUCTS = [(HI, HI), (HI, LO)]
 LO_PRODUCTS = [(LO, HI)]
@@ -68,16 +70,13 @@ def tile_mix_split3_fm_mul_kernel(tc, w, x, g, out):
             return slice(tiles[0], tiles[-1] + 1, step)
 
         half = X_WIDTH // 2
-        x_halves = []
-        for e in range(2):
-            stage = sb.tile([P, PACK, half], F32, name=f"x_half{e}", align_bytes=64)
-            nc.sync.dma_start(out=stage[:], in_=x_rows[:, :, e * half : (e + 1) * half])
-            x_halves.append(stage)
-        x_raw = [None]
-        for i in range(1, X_PIECES):
-            stage = sb.tile([P, PACK, X_WIDTH], F32, name=f"x_raw{i}", align_bytes=64)
-            nc.sync.dma_start(out=stage[:], in_=x_rows[:, :, i * X_WIDTH : (i + 1) * X_WIDTH])
-            x_raw.append(stage)
+        x_place = []
+        for pieces in X_LOADS:
+            first, width = len(x_place) * X_WIDTH, pieces * X_WIDTH
+            stage = sb.tile([P, PACK, width], F32, name=f"x_raw{len(x_place)}", align_bytes=64)
+            nc.sync.dma_start(out=stage[:], in_=x_rows[:, :, first : first + width])
+            x_place.extend((stage, e * X_WIDTH) for e in range(pieces))
+        x_halves = [x_place[0][0][:, :, e * half : (e + 1) * half] for e in range(2)]
         w_place = {}
         g_sb = {}
         for operand, tiles in LOADS:
@@ -102,7 +101,7 @@ def tile_mix_split3_fm_mul_kernel(tc, w, x, g, out):
 
         def x_span(i):
             n = X_WIDTH * PACK
-            return (x_raw[i], 0, X_WIDTH, x_parts[i][:, 0:n], x_parts[i][:, n : 2 * n])
+            return x_place[i] + (X_WIDTH, x_parts[i][:, 0:n], x_parts[i][:, n : 2 * n])
 
         def w_span(c, a0, a1):
             stage, first = w_place[CHUNKS[c][a0]]
@@ -248,19 +247,28 @@ def tile_mix_split3_fm_mul_kernel(tc, w, x, g, out):
                         stop=(w_part, x_part) == LO_PRODUCTS[-1] and t1 == T,
                     )
 
-        def read_out(tiles, t0=0, t1=T):
-            result = sb.tile([P, len(tiles), t1 - t0], F32, name=f"result{tiles[0]}_{t0}", align_bytes=64)
+        results = {}
+        for tiles in STORES:
+            stage = sb.tile([P, len(tiles), T], F32, name=f"result{tiles[0]}", align_bytes=64)
             for t in tiles:
-                nc.vector.tensor_tensor(out=result[:, t - min(tiles), :], in0=sums[t][:, t0:t1], in1=g_sb[t][:, t0:t1], op=ALU.mult)
-            nc.sync.dma_start(out=out_tiles[:, min(tiles) : max(tiles) + 1, t0:t1], in_=result[:])
+                results[t] = (tiles, stage)
+        read = set()
+
+        def read_out(tiles, t0=0, t1=T):
+            for t in tiles:
+                group, stage = results[t]
+                nc.vector.tensor_tensor(out=stage[:, t - group[0], t0:t1], in0=sums[t][:, t0:t1], in1=g_sb[t][:, t0:t1], op=ALU.mult)
+                read.add(t)
+                if all(u in read for u in group):
+                    nc.sync.dma_start(out=out_tiles[:, group[0] : group[-1] + 1, t0:t1], in_=stage[:, :, t0:t1])
 
         n_half = half * PACK
         high0, low0 = x_span(0)[3:]
-        words = [mask_words(f"x_words{e}", x_halves[e][:]) for e in range(2)]
+        words = [mask_words(f"x_words{e}", x_halves[e]) for e in range(2)]
         for e in range(2):
             high_from_words(high0[:, e * n_half : (e + 1) * n_half], words[e])
-            subtract_words(low0[:, e * n_half : (e + 1) * n_half], x_halves[e][:], words[e])
-        words1 = mask_words("x_words_1", x_raw[1][:])
+            subtract_words(low0[:, e * n_half : (e + 1) * n_half], x_halves[e], words[e])
+        words1 = mask_words("x_words_1", raw(x_span(1)))
         truncate(x_span(2))
         truncate(x_span(3))
         high_from_words(x_span(1)[3], words1)
@@ -269,7 +277,7 @@ def tile_mix_split3_fm_mul_kernel(tc, w, x, g, out):
         truncate(w_span(1, 0, 2))
         quantize_x(0, HI)
         quantize_x(0, LO)
-        subtract_words(x_span(1)[4], x_raw[1][:], words1)
+        subtract_words(x_span(1)[4], raw(x_span(1)), words1)
         mask(x_span(2))
         quantize_x(1, LO)
         subtract(x_span(2))
@@ -347,5 +355,4 @@ def tile_mix_split3_fm_mul_kernel(tc, w, x, g, out):
         quantize_w(last, LO)
         multiply(last, LO_PRODUCTS)
         read_out(CHUNKS[last - 1])
-        read_out(CHUNKS[last], 0, T // 2)
-        read_out(CHUNKS[last], T // 2, T)
+        read_out(CHUNKS[last])

@@ -31,13 +31,12 @@ SIDE_BY_SIDE_IN_RUNS = "p (c i j) -> p c j i"
 X_WIDTH = 128
 X_PIECES = T // X_WIDTH
 TURNED_BANKS = 2
-STORES = [[0, 1, 2, 3], [4, 5], [6, 7], [8, 9], [10], [11]]
-X_LOADS = [1, 1, 1, 1]
+STORES = [[0, 1, 2, 3], [4, 5], [6, 7], [8], [9], [10], [11]]
+X_LOADS = [2, 2]
 CHUNKS = [[0, 1], [2, 3], [4, 5], [6, 7], [8, 9], [10], [11]]
-TENSOR_CHUNKS = [3, 4]
+TENSOR_CHUNKS = [3, 4, 6]
 LOADS = [
-    ("w", [0, 1]), ("w", [2, 3]), ("w", [4, 5]), ("w", [6, 7]), ("w", [8, 9]), ("g", [0, 1]),
-    ("g", [2, 3, 4, 5]), ("w", [10, 11]), ("g", [6, 7, 8, 9, 10, 11]),
+    ("w", [0, 1]), ("w", [2, 3]), ("w", [4, 5]), ("w", [6, 7]), ("w", [8, 9]), ("g", [0, 1]), ("w", [10, 11]), ("g", [2, 3]), ("g", [4, 5, 6, 7]), ("g", [8, 9, 10, 11]),
 ]
 HI_PRODUCTS = [(HI, HI), (HI, LO)]
 LO_PRODUCTS = [(LO, HI)]
@@ -111,6 +110,9 @@ def tile_mix_split3_fm_mul_kernel(tc, w, x, g, out):
             low = len(CHUNKS[c]) * n
             return (stage, first, (a1 - a0) * P, w_parts[c][:, a0 * n : a1 * n], w_parts[c][:, low + a0 * n : low + a1 * n])
 
+        def last_tile(c):
+            return w_span(c, len(CHUNKS[c]) - 1, len(CHUNKS[c]))
+
         def raw(span):
             return span[0][:, :, span[1] : span[1] + span[2]]
 
@@ -172,7 +174,7 @@ def tile_mix_split3_fm_mul_kernel(tc, w, x, g, out):
         turned = {}
 
         def mask_negated(chunks):
-            stage, first = w_place[CHUNKS[chunks[0]][1]]
+            stage, first = w_place[CHUNKS[chunks[0]][-1]]
             width = len(chunks) * P
             words = sb.tile([P, PACK, width], F32, name=f"negated{chunks[0]}", align_bytes=64)
             nc.vector.tensor_scalar(
@@ -188,7 +190,7 @@ def tile_mix_split3_fm_mul_kernel(tc, w, x, g, out):
 
         def turn_raw(c):
             turned[c] = psum_turned.tile([P, PACK, P], F32, name="turned")
-            rows = raw(w_span(c, 1, 2))
+            rows = raw(last_tile(c))
             for j in range(PACK):
                 nc.tensor.matmul(turned[c][:, j, :], lhsT=rows[:, j, :], rhs=identity[:], is_transpose=True, start=j == 0, stop=False)
 
@@ -199,7 +201,7 @@ def tile_mix_split3_fm_mul_kernel(tc, w, x, g, out):
                 )
 
         def high_from_negated(c):
-            nc.scalar.activation(out=in_runs(w_span(c, 1, 2)[3]), in_=rows_in_runs(negated[c]), func=ACT.Copy, scale=-1.0)
+            nc.scalar.activation(out=in_runs(last_tile(c)[3]), in_=rows_in_runs(negated[c]), func=ACT.Copy, scale=-1.0)
 
         def round_turned(c):
             pairs = sb.tile([P, PACK * P], BF16, name=f"pairs{c}", align_bytes=64)
@@ -219,7 +221,7 @@ def tile_mix_split3_fm_mul_kernel(tc, w, x, g, out):
 
         def low_from_turned(c):
             nc.scalar.copy(
-                out=w_span(c, 1, 2)[4].bitcast(F32).rearrange("p (n u) -> p n u", u=2),
+                out=last_tile(c)[4].bitcast(F32).rearrange("p (n u) -> p n u", u=2),
                 in_=turned[c].rearrange("p u n -> p n u"),
             )
 
@@ -264,37 +266,40 @@ def tile_mix_split3_fm_mul_kernel(tc, w, x, g, out):
 
         n_half = half * PACK
         high0, low0 = x_span(0)[3:]
+        truncate(x_span(1))
         words = [mask_words(f"x_words{e}", x_halves[e]) for e in range(2)]
         for e in range(2):
             high_from_words(high0[:, e * n_half : (e + 1) * n_half], words[e])
+        for e in range(2):
             subtract_words(low0[:, e * n_half : (e + 1) * n_half], x_halves[e], words[e])
-        words1 = mask_words("x_words_1", raw(x_span(1)))
         truncate(x_span(2))
         truncate(x_span(3))
-        high_from_words(x_span(1)[3], words1)
         truncate(w_span(0, 0, 1))
         truncate(w_span(0, 1, 2))
         truncate(w_span(1, 0, 2))
-        quantize_x(0, HI)
+        mask(x_span(1))
         quantize_x(0, LO)
-        subtract_words(x_span(1)[4], raw(x_span(1)), words1)
+        subtract(x_span(1))
+        quantize_x(0, HI)
+        quantize_x(1, HI)
         mask(x_span(2))
         quantize_x(1, LO)
         subtract(x_span(2))
         mask(x_span(3))
         quantize_x(2, HI)
-        quantize_x(1, HI)
+        quantize_x(2, LO)
         subtract(x_span(3))
         mask(w_span(0, 0, 1))
-        quantize_x(2, LO)
         quantize_x(3, HI)
-        quantize_w_tile(0, 0, HI)
-        mask(w_span(0, 1, 2))
         quantize_x(3, LO)
+        quantize_w_tile(0, 0, HI)
         multiply(0, HI_PRODUCTS, only=0)
+        mask(w_span(0, 1, 2))
+        subtract(w_span(0, 0, 1))
         quantize_w_tile(0, 1, HI)
         multiply(0, HI_PRODUCTS, only=1)
-        subtract(w_span(0, 0, 2))
+        subtract(w_span(0, 1, 2))
+
         def masked(c):
             return w_span(c, 0, 1 if c in TENSOR_CHUNKS else len(CHUNKS[c]))
 
@@ -314,21 +319,24 @@ def tile_mix_split3_fm_mul_kernel(tc, w, x, g, out):
         last = len(CHUNKS) - 1
         order = [t for c, ts in enumerate(CHUNKS) for t in (ts[::-1] if c in TENSOR_CHUNKS else ts)]
         done = 0
-        for c in range(2, last + 1):
-            if c + 2 in TENSOR_CHUNKS:
-                mask_negated([c + 2])
-            if c in TENSOR_CHUNKS:
-                turn_back([c])
-                low_from_turned(c)
+        for c in range(2, last):
+            starts = {2: 4, 3: last}.get(c)
+            returns = {3: [3], 4: [4, last]}.get(c, [])
+            if starts:
+                mask_negated([starts])
+            if returns:
+                turn_back(returns)
+            for r in returns:
+                low_from_turned(r)
             if c + 1 in TENSOR_CHUNKS:
                 high_from_negated(c + 1)
-            if c + 2 <= last:
+            if starts:
+                turn_raw(starts)
+                turn_negated(starts)
+                round_turned(starts)
+            if c + 2 < last:
                 lay_out(c + 2)
                 truncate(masked(c + 2))
-            if c + 2 in TENSOR_CHUNKS:
-                turn_raw(c + 2)
-                turn_negated(c + 2)
-                round_turned(c + 2)
             split_call = c - 1 in TENSOR_CHUNKS
             if split_call:
                 quantize_slots(c - 1, 2, 4)
@@ -341,18 +349,13 @@ def tile_mix_split3_fm_mul_kernel(tc, w, x, g, out):
             else:
                 quantize_slots(c - 1, 0, 2 * len(CHUNKS[c - 1]))
                 multiply(c - 1, all_products)
-            if c == last:
-                quantize_w(last, HI)
-                multiply(last, HI_PRODUCTS)
-            if c < last:
-                read_out(order[done : done + 2])
-            else:
-                read_out(order[done : done + 1])
-                read_out(order[done + 1 : done + 2])
+            read_out(order[done : done + 2])
             done = done + 2
             if len(CHUNKS[c]) > 1 and c not in TENSOR_CHUNKS:
                 subtract(w_span(c, 1, 2))
-        quantize_w(last, LO)
-        multiply(last, LO_PRODUCTS)
+        for c in (last, last - 1):
+            quantize_slots(c, 0, 2)
+            multiply(c, all_products)
+        for t in order[done : done + 2] + CHUNKS[last]:
+            read_out([t])
         read_out(CHUNKS[last - 1])
-        read_out(CHUNKS[last])

@@ -18,37 +18,43 @@ ACT = mybir.ActivationFunctionType
 P = 128
 PACK = 4
 HI, LO = 0, 1
-SUM_BANKS = 5
-SIGN_BIT = -(1 << 31)
+MX_ALIGN = 64
+DMA_ALIGN = 256
+
+SUM_BANKS, TURNED_BANKS, BACK_BANKS = 5, 2, 1
 
 WORD_MASK = 0xFFF00000 - (1 << 32)
 PAIR_MASK = 0xFFF0FFF0 - (1 << 32)
+SIGN_BIT = -(1 << 31)
 
 RUN = 2
 ROWS_IN_RUNS = "p j (c i) -> p c j i"
 SIDE_BY_SIDE_IN_RUNS = "p (c i j) -> p c j i"
 
-X_WIDTH = 128
-X_PIECES = T // X_WIDTH
-TURNED_BANKS = 2
-STORES = [[0, 1, 2, 3], [4, 5], [6, 7], [8], [9], [10], [11]]
-X_LOADS = [2, 2]
 CHUNKS = [[0, 1], [2, 3], [4, 5], [6, 7], [8, 9], [10], [11]]
-TENSOR_CHUNKS = [3, 4, 6]
+LAST = len(CHUNKS) - 1
+TENSOR_CHUNKS = [3, 4, LAST]
+TENSOR_STARTS = {1: 3, 2: 4, 3: LAST}
+TENSOR_RETURNS = {3: [3], 4: [4, LAST]}
+
 LOADS = [
-    ("w", [0, 1]), ("w", [2, 3]), ("w", [4, 5]), ("w", [6, 7]), ("w", [8, 9]), ("g", [0, 1]), ("w", [10, 11]), ("g", [2, 3]), ("g", [4, 5, 6, 7]), ("g", [8, 9, 10, 11]),
+    ("x", 0, 1), ("x", 1, 1), ("x", 2, 2), ("w", 0, 2), ("w", 2, 2), ("w", 4, 4), ("w", 8, 2),
+    ("g", 0, 2), ("w", 10, 2), ("g", 2, 2), ("g", 4, 4), ("g", 8, 4),
 ]
+STORES = [(0, 4), (4, 2), (6, 2), (8, 1), (9, 1), (10, 1), (11, 1)]
+
 HI_PRODUCTS = [(HI, HI), (HI, LO)]
 LO_PRODUCTS = [(LO, HI)]
+ALL_PRODUCTS = HI_PRODUCTS + LO_PRODUCTS
 
 
 def tile_mix_split3_fm_mul_kernel(tc, w, x, g, out):
     nc = tc.nc
     with ExitStack() as ctx:
         sb = ctx.enter_context(tc.tile_pool(name="sb", bufs=1))
-        psum = ctx.enter_context(tc.psum_pool(name="psum", bufs=SUM_BANKS))
+        psum_sums = ctx.enter_context(tc.psum_pool(name="psum_sums", bufs=SUM_BANKS))
         psum_turned = ctx.enter_context(tc.psum_pool(name="psum_turned", bufs=TURNED_BANKS))
-        psum_back = ctx.enter_context(tc.psum_pool(name="psum_back", bufs=1))
+        psum_back = ctx.enter_context(tc.psum_pool(name="psum_back", bufs=BACK_BANKS))
         ctx.enter_context(tc.manual_schedule())
 
         warm_in = sb.tile([P, 2], BF16, name="warm_in")
@@ -56,62 +62,59 @@ def tile_mix_split3_fm_mul_kernel(tc, w, x, g, out):
         nc.vector.memset(warm_in[:], 0.0)
         nc.scalar.copy(out=warm_out[:], in_=warm_in[:])
 
-        identity = sb.tile([P, P], F32, name="identity", align_bytes=64)
+        identity = sb.tile([P, P], F32, name="identity", align_bytes=MX_ALIGN)
         make_identity(nc, identity[:])
 
-        x_rows = x.rearrange("(p j) t -> p j t", j=PACK)
-        w_rows = w.rearrange("(p j) n -> p j n", j=PACK)
+        k_rows = {"x": x.rearrange("(p j) t -> p j t", j=PACK), "w": w.rearrange("(p j) n -> p j n", j=PACK)}
         g_tiles = g.rearrange("(a p) t -> p a t", p=P)
         out_tiles = out.rearrange("(a p) t -> p a t", p=P)
-
-        def stepped(tiles):
-            step = tiles[1] - tiles[0] if len(tiles) > 1 else 1
-            return slice(tiles[0], tiles[-1] + 1, step)
-
-        half = X_WIDTH // 2
-        x_place = []
-        for pieces in X_LOADS:
-            first, width = len(x_place) * X_WIDTH, pieces * X_WIDTH
-            stage = sb.tile([P, PACK, width], F32, name=f"x_raw{len(x_place)}", align_bytes=64)
-            nc.sync.dma_start(out=stage[:], in_=x_rows[:, :, first : first + width])
-            x_place.extend((stage, e * X_WIDTH) for e in range(pieces))
-        x_halves = [x_place[0][0][:, :, e * half : (e + 1) * half] for e in range(2)]
-        w_place = {}
+        place = {}
         g_sb = {}
-        for operand, tiles in LOADS:
-            if operand == "w":
-                stage = sb.tile([P, PACK, len(tiles) * P], F32, name=f"w_raw{tiles[0]}", align_bytes=64)
-                nc.sync.dma_start(out=stage[:], in_=w_rows[:, :, tiles[0] * P : (tiles[-1] + 1) * P])
-                for a, t in enumerate(tiles):
-                    w_place[t] = (stage, a * P)
+        for operand, first, count in LOADS:
+            if operand == "g":
+                stage = sb.tile([P, count, T], F32, name=f"g_sb{first}", align_bytes=DMA_ALIGN)
+                nc.sync.dma_start(out=stage[:], in_=g_tiles[:, first : first + count, :])
+                for a in range(count):
+                    g_sb[first + a] = stage[:, a, :]
             else:
-                stage = sb.tile([P, len(tiles), T], F32, name=f"g_sb{tiles[0]}", align_bytes=64)
-                nc.sync.dma_start(out=stage[:], in_=g_tiles[:, stepped(tiles), :])
-                for a, t in enumerate(tiles):
-                    g_sb[t] = stage[:, a, :]
+                stage = sb.tile([P, PACK, count * P], F32, name=f"{operand}_raw{first}", align_bytes=DMA_ALIGN)
+                nc.sync.dma_start(out=stage[:], in_=k_rows[operand][:, :, first * P : (first + count) * P])
+                for a in range(count):
+                    place[operand, first + a] = (stage, a * P)
+        results = {}
+        for first, count in STORES:
+            stage = sb.tile([P, count, T], F32, name=f"result{first}", align_bytes=DMA_ALIGN)
+            for a in range(count):
+                results[first + a] = (first, count, stage)
 
-        x_parts = [sb.tile([P, 2 * X_WIDTH * PACK], BF16, name=f"x_parts{i}", align_bytes=64) for i in range(X_PIECES)]
-        w_parts = [sb.tile([P, 2 * len(ts) * P * PACK], BF16, name=f"w_parts{c}", align_bytes=64) for c, ts in enumerate(CHUNKS)]
-        x_codes = sb.tile([P, 2, T], U32, name="x_codes", align_bytes=64)
-        x_scales = sb.tile([P, 2, T], U8, name="x_scales", align_bytes=64)
-        w_codes = [sb.tile([P, 2 * len(ts) * P], U32, name=f"w_codes{c}", align_bytes=64) for c, ts in enumerate(CHUNKS)]
-        w_scales = [sb.tile([P, 2 * len(ts) * P], U8, name=f"w_scales{c}", align_bytes=64) for c, ts in enumerate(CHUNKS)]
-        sums = {}
+        slot_size = P * PACK
+        x_parts = [sb.tile([P, T * PACK], BF16, name=f"x_parts{h}", align_bytes=MX_ALIGN) for h in (HI, LO)]
+        x_codes = sb.tile([P, 2, T], U32, name="x_codes", align_bytes=MX_ALIGN)
+        x_scales = sb.tile([P, 2, T], U8, name="x_scales", align_bytes=MX_ALIGN)
+        w_parts, w_codes, w_scales = [], [], []
+        for c, tiles in enumerate(CHUNKS):
+            slots = 2 * len(tiles)
+            w_parts.append(sb.tile([P, slots * slot_size], BF16, name=f"w_parts{c}", align_bytes=MX_ALIGN))
+            w_codes.append(sb.tile([P, slots * P], U32, name=f"w_codes{c}", align_bytes=MX_ALIGN))
+            w_scales.append(sb.tile([P, slots * P], U8, name=f"w_scales{c}", align_bytes=MX_ALIGN))
+
+        def slot(c, a, h):
+            return 2 * a + h if c in TENSOR_CHUNKS else h * len(CHUNKS[c]) + a
 
         def x_span(i):
-            n = X_WIDTH * PACK
-            return x_place[i] + (X_WIDTH, x_parts[i][:, 0:n], x_parts[i][:, n : 2 * n])
+            cols = slice(i * slot_size, (i + 1) * slot_size)
+            return place["x", i] + (P, x_parts[HI][:, cols], x_parts[LO][:, cols])
 
-        def w_span(c, a0, a1):
-            stage, first = w_place[CHUNKS[c][a0]]
-            n = P * PACK
-            if c in TENSOR_CHUNKS:
-                return (stage, first, P, w_parts[c][:, 2 * a0 * n : (2 * a0 + 1) * n], w_parts[c][:, (2 * a0 + 1) * n : (2 * a0 + 2) * n])
-            low = len(CHUNKS[c]) * n
-            return (stage, first, (a1 - a0) * P, w_parts[c][:, a0 * n : a1 * n], w_parts[c][:, low + a0 * n : low + a1 * n])
+        def w_span(c, a, count=1):
+            high, low = slot(c, a, HI) * slot_size, slot(c, a, LO) * slot_size
+            size = count * slot_size
+            return place["w", CHUNKS[c][a]] + (count * P, w_parts[c][:, high : high + size], w_parts[c][:, low : low + size])
 
-        def last_tile(c):
-            return w_span(c, len(CHUNKS[c]) - 1, len(CHUNKS[c]))
+        def paired(c):
+            return w_span(c, 0, 1 if c in TENSOR_CHUNKS else len(CHUNKS[c]))
+
+        def tensor_tile(c):
+            return w_span(c, len(CHUNKS[c]) - 1)
 
         def raw(span):
             return span[0][:, :, span[1] : span[1] + span[2]]
@@ -123,9 +126,9 @@ def tile_mix_split3_fm_mul_kernel(tc, w, x, g, out):
             return part.rearrange(SIDE_BY_SIDE_IN_RUNS, i=RUN, j=PACK)
 
         def truncate(span):
-            stage, first, width = span[:3]
+            stage, first, width, high = span[:4]
             halves = stage[:].bitcast(BF16).rearrange("p j (c i h) -> p c j i h", i=RUN, h=2)
-            nc.scalar.copy(out=in_runs(span[3]), in_=halves[:, first // RUN : (first + width) // RUN, :, :, 1])
+            nc.scalar.copy(out=in_runs(high), in_=halves[:, first // RUN : (first + width) // RUN, :, :, 1])
 
         def mask(span):
             words = span[3].bitcast(I32)
@@ -134,228 +137,185 @@ def tile_mix_split3_fm_mul_kernel(tc, w, x, g, out):
         def subtract(span):
             nc.vector.tensor_tensor(out=in_runs(span[4]), in0=rows_in_runs(raw(span)), in1=in_runs(span[3]), op=ALU.subtract)
 
-        def mask_words(name, rows):
-            words = sb.tile(list(rows.shape), F32, name=name, align_bytes=64)
-            nc.vector.tensor_scalar(
-                out=words[:].bitcast(I32), in0=rows.bitcast(I32), scalar1=WORD_MASK, scalar2=None, op0=ALU.bitwise_and
-            )
-            return words
-
-        def subtract_words(low, rows, words):
-            nc.vector.tensor_tensor(out=in_runs(low), in0=rows_in_runs(rows), in1=rows_in_runs(words[:]), op=ALU.subtract)
-
-        def high_from_words(high, words):
-            nc.scalar.copy(out=in_runs(high), in_=rows_in_runs(words[:]))
-
-        def slot(c, a, h):
-            return 2 * a + h if c in TENSOR_CHUNKS else h * len(CHUNKS[c]) + a
-
-        def quantize_slots(c, s0, s1):
-            nc.vector.quantize_mx(
-                out=w_codes[c][:, s0 * P : s1 * P].bitcast(FP8X4),
-                scales=w_scales[c][:, s0 * P : s1 * P],
-                in_=w_parts[c][:, s0 * P * PACK : s1 * P * PACK],
-            )
-
-        def quantize_w_tile(c, a, h):
-            quantize_slots(c, slot(c, a, h), slot(c, a, h) + 1)
-
         laid_out = {}
 
-        def lay_out(c):
-            laid_out[c] = sb.tile([P, P * PACK], F32, name=f"rows{c}", align_bytes=64)
-            nc.scalar.copy(out=in_runs(laid_out[c][:]), in_=rows_in_runs(raw(w_span(c, 0, 1))))
+        def prepare(c):
+            laid_out[c] = sb.tile([P, slot_size], F32, name=f"laid_out{c}", align_bytes=MX_ALIGN)
+            nc.scalar.copy(out=in_runs(laid_out[c][:]), in_=rows_in_runs(raw(w_span(c, 0))))
+            truncate(paired(c))
 
         def subtract_on_gpsimd(c):
-            span = w_span(c, 0, 1)
-            nc.gpsimd.tensor_tensor(out=span[4], in0=laid_out[c][:], in1=span[3], op=ALU.subtract)
+            high, low = w_span(c, 0)[3:]
+            nc.gpsimd.tensor_tensor(out=low, in0=laid_out[c][:], in1=high, op=ALU.subtract)
 
         negated = {}
         turned = {}
+        rounded = {}
+        back = {}
 
-        def mask_negated(chunks):
-            stage, first = w_place[CHUNKS[chunks[0]][-1]]
-            width = len(chunks) * P
-            words = sb.tile([P, PACK, width], F32, name=f"negated{chunks[0]}", align_bytes=64)
+        def mask_negated(c):
+            negated[c] = sb.tile([P, PACK, P], F32, name=f"negated{c}", align_bytes=MX_ALIGN)
             nc.vector.tensor_scalar(
-                out=words[:].bitcast(I32),
-                in0=stage[:, :, first : first + width].bitcast(I32),
+                out=negated[c][:].bitcast(I32),
+                in0=raw(tensor_tile(c)).bitcast(I32),
                 scalar1=WORD_MASK,
                 scalar2=SIGN_BIT,
                 op0=ALU.bitwise_and,
                 op1=ALU.bitwise_xor,
             )
-            for a, c in enumerate(chunks):
-                negated[c] = words[:, :, a * P : (a + 1) * P]
 
-        def turn_raw(c):
+        def subtract_on_tensor(c):
             turned[c] = psum_turned.tile([P, PACK, P], F32, name="turned")
-            rows = raw(last_tile(c))
-            for j in range(PACK):
-                nc.tensor.matmul(turned[c][:, j, :], lhsT=rows[:, j, :], rhs=identity[:], is_transpose=True, start=j == 0, stop=False)
-
-        def turn_negated(c):
-            for j in range(PACK):
-                nc.tensor.matmul(
-                    turned[c][:, j, :], lhsT=negated[c][:, j, :], rhs=identity[:], is_transpose=True, start=False, stop=j == PACK - 1
-                )
-
-        def high_from_negated(c):
-            nc.scalar.activation(out=in_runs(last_tile(c)[3]), in_=rows_in_runs(negated[c]), func=ACT.Copy, scale=-1.0)
+            terms = [raw(tensor_tile(c)), negated[c][:]]
+            for s, rows in enumerate(terms):
+                for j in range(PACK):
+                    nc.tensor.matmul(
+                        turned[c][:, j, :],
+                        lhsT=rows[:, j, :],
+                        rhs=identity[:],
+                        is_transpose=True,
+                        start=s == 0 and j == 0,
+                        stop=s == len(terms) - 1 and j == PACK - 1,
+                    )
 
         def round_turned(c):
-            pairs = sb.tile([P, PACK * P], BF16, name=f"pairs{c}", align_bytes=64)
+            rounded[c] = sb.tile([P, slot_size], BF16, name=f"rounded{c}", align_bytes=MX_ALIGN)
             nc.scalar.copy(
-                out=pairs[:].rearrange("n (u p e) -> n u p e", u=2, e=2),
+                out=rounded[c][:].rearrange("n (u p e) -> n u p e", u=2, e=2),
                 in_=turned[c][:].rearrange("n (u e) p -> n u p e", e=2),
             )
-            turned[c] = pairs
 
         def turn_back(chunks):
             bank = psum_back.tile([P, 2, 2, P], F32, name="back")
             for a, c in enumerate(chunks):
-                words = turned[c][:].bitcast(F32)
+                words = rounded[c][:].bitcast(F32)
                 for u in range(2):
                     nc.tensor.transpose(bank[:, a, u, :], words[:, u * P : (u + 1) * P], identity[:])
-                turned[c] = bank[:, a, :, :]
+                back[c] = bank[:, a, :, :]
 
-        def low_from_turned(c):
+        def low_from_back(c):
             nc.scalar.copy(
-                out=last_tile(c)[4].bitcast(F32).rearrange("p (n u) -> p n u", u=2),
-                in_=turned[c].rearrange("p u n -> p n u"),
+                out=tensor_tile(c)[4].bitcast(F32).rearrange("p (n u) -> p n u", u=2),
+                in_=back[c].rearrange("p u n -> p n u"),
             )
 
-        def quantize_x(i, h):
-            cols = slice(i * X_WIDTH, (i + 1) * X_WIDTH)
-            nc.vector.quantize_mx(out=x_codes[:, h, cols].bitcast(FP8X4), scales=x_scales[:, h, cols], in_=x_span(i)[3 + h])
+        def high_from_negated(c):
+            nc.scalar.activation(out=in_runs(tensor_tile(c)[3]), in_=rows_in_runs(negated[c][:]), func=ACT.Copy, scale=-1.0)
 
-        def quantize_w(c, h):
-            quantize_slots(c, slot(c, 0, h), slot(c, 0, h) + len(CHUNKS[c]))
+        def quantize_x(first, count, h):
+            t0, t1 = first * P, (first + count) * P
+            nc.vector.quantize_mx(
+                out=x_codes[:, h, t0:t1].bitcast(FP8X4), scales=x_scales[:, h, t0:t1], in_=x_parts[h][:, t0 * PACK : t1 * PACK]
+            )
 
-        def multiply(c, products, t0=0, t1=T, only=None):
-            for a, t in enumerate(CHUNKS[c]):
-                for w_part, x_part in products if only in (None, a) else []:
-                    cols = slice(slot(c, a, w_part) * P, (slot(c, a, w_part) + 1) * P)
-                    opens = (w_part, x_part) == HI_PRODUCTS[0] and t0 == 0
-                    if opens:
-                        sums[t] = psum.tile([P, T], F32, name="sums")
-                    nc.tensor.matmul_mx(
-                        out=sums[t][:, t0:t1],
-                        lhsT=w_codes[c][:, cols].bitcast(FP8X4),
-                        lhsT_scale=w_scales[c][:, cols],
-                        rhs=x_codes[:, x_part, t0:t1].bitcast(FP8X4),
-                        rhs_scale=x_scales[:, x_part, t0:t1],
-                        start=opens,
-                        stop=(w_part, x_part) == LO_PRODUCTS[-1] and t1 == T,
-                    )
+        def quantize_slots(c, first, count):
+            n0, n1 = first * P, (first + count) * P
+            nc.vector.quantize_mx(
+                out=w_codes[c][:, n0:n1].bitcast(FP8X4), scales=w_scales[c][:, n0:n1], in_=w_parts[c][:, n0 * PACK : n1 * PACK]
+            )
 
-        results = {}
-        for tiles in STORES:
-            stage = sb.tile([P, len(tiles), T], F32, name=f"result{tiles[0]}", align_bytes=64)
-            for t in tiles:
-                results[t] = (tiles, stage)
+        sums = {}
+
+        def multiply(c, a, products):
+            t = CHUNKS[c][a]
+            for w_part, x_part in products:
+                opens = (w_part, x_part) == ALL_PRODUCTS[0]
+                if opens:
+                    sums[t] = psum_sums.tile([P, T], F32, name="sums")
+                cols = slice(slot(c, a, w_part) * P, (slot(c, a, w_part) + 1) * P)
+                nc.tensor.matmul_mx(
+                    out=sums[t][:],
+                    lhsT=w_codes[c][:, cols].bitcast(FP8X4),
+                    lhsT_scale=w_scales[c][:, cols],
+                    rhs=x_codes[:, x_part, :].bitcast(FP8X4),
+                    rhs_scale=x_scales[:, x_part, :],
+                    start=opens,
+                    stop=(w_part, x_part) == ALL_PRODUCTS[-1],
+                )
+
+        def quantize_and_multiply_tile(c, a):
+            quantize_slots(c, slot(c, a, HI), 2)
+            multiply(c, a, ALL_PRODUCTS)
+
         read = set()
 
-        def read_out(tiles, t0=0, t1=T):
-            for t in tiles:
-                group, stage = results[t]
-                nc.vector.tensor_tensor(out=stage[:, t - group[0], t0:t1], in0=sums[t][:, t0:t1], in1=g_sb[t][:, t0:t1], op=ALU.mult)
+        def read_out(c):
+            for t in reversed(CHUNKS[c]) if c in TENSOR_CHUNKS else CHUNKS[c]:
+                first, count, stage = results[t]
+                nc.vector.tensor_tensor(out=stage[:, t - first, :], in0=sums[t][:], in1=g_sb[t], op=ALU.mult)
                 read.add(t)
-                if all(u in read for u in group):
-                    nc.sync.dma_start(out=out_tiles[:, group[0] : group[-1] + 1, t0:t1], in_=stage[:, :, t0:t1])
+                if all(first + a in read for a in range(count)):
+                    nc.sync.dma_start(out=out_tiles[:, first : first + count, :], in_=stage[:])
 
-        n_half = half * PACK
-        high0, low0 = x_span(0)[3:]
+        first_rows = raw(x_span(0))
+        first_high = sb.tile([P, PACK, P], F32, name="first_high", align_bytes=MX_ALIGN)
+        nc.vector.tensor_scalar(
+            out=first_high[:].bitcast(I32), in0=first_rows.bitcast(I32), scalar1=WORD_MASK, scalar2=None, op0=ALU.bitwise_and
+        )
+        nc.vector.tensor_tensor(
+            out=in_runs(x_span(0)[4]), in0=rows_in_runs(first_rows), in1=rows_in_runs(first_high[:]), op=ALU.subtract
+        )
         truncate(x_span(1))
-        words = [mask_words(f"x_words{e}", x_halves[e]) for e in range(2)]
-        for e in range(2):
-            high_from_words(high0[:, e * n_half : (e + 1) * n_half], words[e])
-        for e in range(2):
-            subtract_words(low0[:, e * n_half : (e + 1) * n_half], x_halves[e], words[e])
-        truncate(x_span(2))
-        truncate(x_span(3))
-        truncate(w_span(0, 0, 1))
-        truncate(w_span(0, 1, 2))
-        truncate(w_span(1, 0, 2))
+        nc.scalar.copy(out=in_runs(x_span(0)[3]), in_=rows_in_runs(first_high[:]))
+        for span in (x_span(2), x_span(3), paired(0), paired(1)):
+            truncate(span)
         mask(x_span(1))
-        quantize_x(0, LO)
         subtract(x_span(1))
-        quantize_x(0, HI)
-        quantize_x(1, HI)
+        quantize_x(0, 2, HI)
         mask(x_span(2))
-        quantize_x(1, LO)
-        subtract(x_span(2))
+        quantize_x(0, 2, LO)
         mask(x_span(3))
-        quantize_x(2, HI)
-        quantize_x(2, LO)
+        subtract(x_span(2))
         subtract(x_span(3))
-        mask(w_span(0, 0, 1))
-        quantize_x(3, HI)
-        quantize_x(3, LO)
-        quantize_w_tile(0, 0, HI)
-        multiply(0, HI_PRODUCTS, only=0)
-        mask(w_span(0, 1, 2))
-        subtract(w_span(0, 0, 1))
-        quantize_w_tile(0, 1, HI)
-        multiply(0, HI_PRODUCTS, only=1)
-        subtract(w_span(0, 1, 2))
+        quantize_x(2, 2, HI)
 
-        def masked(c):
-            return w_span(c, 0, 1 if c in TENSOR_CHUNKS else len(CHUNKS[c]))
+        mask(paired(0))
+        quantize_x(2, 2, LO)
+        quantize_slots(0, slot(0, 0, HI), 2)
+        for a in range(2):
+            multiply(0, a, HI_PRODUCTS)
+        subtract(paired(0))
+        prepare(2)
+        prepare(3)
 
-        lay_out(2)
-        truncate(masked(2))
-        lay_out(3)
-        truncate(masked(3))
-        mask(masked(1))
-        mask_negated([3])
-        quantize_w(0, LO)
-        subtract(masked(1))
-        turn_raw(3)
-        turn_negated(3)
-        multiply(0, LO_PRODUCTS)
-        round_turned(3)
-        all_products = HI_PRODUCTS + LO_PRODUCTS
-        last = len(CHUNKS) - 1
-        order = [t for c, ts in enumerate(CHUNKS) for t in (ts[::-1] if c in TENSOR_CHUNKS else ts)]
-        done = 0
-        for c in range(2, last):
-            starts = {2: 4, 3: last}.get(c)
-            returns = {3: [3], 4: [4, last]}.get(c, [])
-            if starts:
-                mask_negated([starts])
-            if returns:
-                turn_back(returns)
-            for r in returns:
-                low_from_turned(r)
+        mask(paired(1))
+        mask_negated(TENSOR_STARTS[1])
+        quantize_slots(0, slot(0, 0, LO), 2)
+        subtract(paired(1))
+        subtract_on_tensor(TENSOR_STARTS[1])
+        for a in range(2):
+            multiply(0, a, LO_PRODUCTS)
+        round_turned(TENSOR_STARTS[1])
+
+        for c in range(2, LAST):
+            if c in TENSOR_STARTS:
+                mask_negated(TENSOR_STARTS[c])
+            if c in TENSOR_RETURNS:
+                turn_back(TENSOR_RETURNS[c])
+                for returning in TENSOR_RETURNS[c]:
+                    low_from_back(returning)
             if c + 1 in TENSOR_CHUNKS:
                 high_from_negated(c + 1)
-            if starts:
-                turn_raw(starts)
-                turn_negated(starts)
-                round_turned(starts)
-            if c + 2 < last:
-                lay_out(c + 2)
-                truncate(masked(c + 2))
-            split_call = c - 1 in TENSOR_CHUNKS
-            if split_call:
-                quantize_slots(c - 1, 2, 4)
-                multiply(c - 1, all_products, only=1)
-            mask(masked(c))
+            if c in TENSOR_STARTS:
+                subtract_on_tensor(TENSOR_STARTS[c])
+                round_turned(TENSOR_STARTS[c])
+            if c + 2 < LAST:
+                prepare(c + 2)
+            if c - 1 in TENSOR_CHUNKS:
+                quantize_and_multiply_tile(c - 1, 1)
+            mask(paired(c))
             subtract_on_gpsimd(c)
-            if split_call:
-                quantize_slots(c - 1, 0, 2)
-                multiply(c - 1, all_products, only=0)
+            if c - 1 in TENSOR_CHUNKS:
+                quantize_and_multiply_tile(c - 1, 0)
             else:
-                quantize_slots(c - 1, 0, 2 * len(CHUNKS[c - 1]))
-                multiply(c - 1, all_products)
-            read_out(order[done : done + 2])
-            done = done + 2
-            if len(CHUNKS[c]) > 1 and c not in TENSOR_CHUNKS:
-                subtract(w_span(c, 1, 2))
-        for c in (last, last - 1):
-            quantize_slots(c, 0, 2)
-            multiply(c, all_products)
-        for t in order[done : done + 2] + CHUNKS[last]:
-            read_out([t])
-        read_out(CHUNKS[last - 1])
+                quantize_slots(c - 1, 0, 4)
+                for a in range(2):
+                    multiply(c - 1, a, ALL_PRODUCTS)
+            read_out(c - 2)
+            if len(CHUNKS[c]) == 2 and c not in TENSOR_CHUNKS:
+                subtract(w_span(c, 1))
+
+        for c in (LAST, LAST - 1):
+            quantize_and_multiply_tile(c, 0)
+        for c in (LAST - 2, LAST, LAST - 1):
+            read_out(c)

@@ -33,12 +33,12 @@ SIDE_BY_SIDE_IN_RUNS = "p (c i j) -> p c j i"
 
 CHUNKS = [[0, 1], [2, 3], [4, 5], [6, 7], [8, 9], [10], [11]]
 LAST = len(CHUNKS) - 1
-TENSOR_CHUNKS = [3, 4, LAST]
-TENSOR_STARTS = {1: 3, 2: 4, 3: LAST}
-TENSOR_RETURNS = {3: [3], 4: [4, LAST]}
+TENSOR_CHUNKS = [2, 4, LAST]
+TENSOR_STARTS = {0: 2, 2: 4, 3: LAST}
+TENSOR_RETURNS = {2: [2], 4: [4, LAST]}
 
 LOADS = [
-    ("x", 0, 1), ("x", 1, 1), ("x", 2, 2), ("w", 0, 2), ("w", 2, 2), ("w", 4, 4), ("w", 8, 2),
+    ("x", 0, 1), ("x", 1, 1), ("x", 2, 2), ("w", 0, 2), ("w", 4, 2), ("w", 2, 2), ("w", 6, 4),
     ("g", 0, 2), ("w", 10, 2), ("g", 2, 2), ("g", 4, 4), ("g", 8, 4),
 ]
 STORES = [(0, 4), (4, 2), (6, 2), (8, 1), (9, 1), (10, 1), (11, 1)]
@@ -247,26 +247,32 @@ def tile_mix_split3_fm_mul_kernel(tc, w, x, g, out):
                 if all(first + a in read for a in range(count)):
                     nc.sync.dma_start(out=out_tiles[:, first : first + count, :], in_=stage[:])
 
-        first_rows = raw(x_span(0))
-        first_high = sb.tile([P, PACK, P], F32, name="first_high", align_bytes=MX_ALIGN)
-        nc.vector.tensor_scalar(
-            out=first_high[:].bitcast(I32), in0=first_rows.bitcast(I32), scalar1=WORD_MASK, scalar2=None, op0=ALU.bitwise_and
-        )
-        nc.vector.tensor_tensor(
-            out=in_runs(x_span(0)[4]), in0=rows_in_runs(first_rows), in1=rows_in_runs(first_high[:]), op=ALU.subtract
-        )
-        truncate(x_span(1))
-        nc.scalar.copy(out=in_runs(x_span(0)[3]), in_=rows_in_runs(first_high[:]))
-        for span in (x_span(2), x_span(3), paired(0), paired(1)):
+        word_highs = []
+        for i in range(2):
+            words = sb.tile([P, PACK, P], F32, name=f"word_high{i}", align_bytes=MX_ALIGN)
+            nc.vector.tensor_scalar(
+                out=words[:].bitcast(I32), in0=raw(x_span(i)).bitcast(I32), scalar1=WORD_MASK, scalar2=None, op0=ALU.bitwise_and
+            )
+            nc.scalar.copy(out=in_runs(x_span(i)[3]), in_=rows_in_runs(words[:]))
+            word_highs.append(words)
+        for i in range(2):
+            nc.vector.tensor_tensor(
+                out=in_runs(x_span(i)[4]), in0=rows_in_runs(raw(x_span(i))), in1=rows_in_runs(word_highs[i][:]), op=ALU.subtract
+            )
+        for span in (x_span(2), x_span(3), paired(0)):
             truncate(span)
-        mask(x_span(1))
-        subtract(x_span(1))
+        prepare(2)
+        truncate(paired(1))
         quantize_x(0, 2, HI)
         mask(x_span(2))
         quantize_x(0, 2, LO)
         mask(x_span(3))
         subtract(x_span(2))
         subtract(x_span(3))
+        mask_negated(TENSOR_STARTS[0])
+        subtract_on_tensor(TENSOR_STARTS[0])
+        high_from_negated(TENSOR_STARTS[0])
+        round_turned(TENSOR_STARTS[0])
         quantize_x(2, 2, HI)
 
         mask(paired(0))
@@ -275,17 +281,13 @@ def tile_mix_split3_fm_mul_kernel(tc, w, x, g, out):
         for a in range(2):
             multiply(0, a, HI_PRODUCTS)
         subtract(paired(0))
-        prepare(2)
         prepare(3)
 
         mask(paired(1))
-        mask_negated(TENSOR_STARTS[1])
         quantize_slots(0, slot(0, 0, LO), 2)
         subtract(paired(1))
-        subtract_on_tensor(TENSOR_STARTS[1])
         for a in range(2):
             multiply(0, a, LO_PRODUCTS)
-        round_turned(TENSOR_STARTS[1])
 
         for c in range(2, LAST):
             if c in TENSOR_STARTS:
@@ -317,5 +319,10 @@ def tile_mix_split3_fm_mul_kernel(tc, w, x, g, out):
 
         for c in (LAST, LAST - 1):
             quantize_and_multiply_tile(c, 0)
-        for c in (LAST - 2, LAST, LAST - 1):
+        for c in (LAST - 2, LAST):
             read_out(c)
+        t = CHUNKS[LAST - 1][0]
+        stage = results[t][2]
+        for half in (slice(0, T // 2), slice(T // 2, T)):
+            nc.vector.tensor_tensor(out=stage[:, 0, half], in0=sums[t][:, half], in1=g_sb[t][:, half], op=ALU.mult)
+            nc.sync.dma_start(out=out_tiles[:, t, half], in_=stage[:, 0, half])

@@ -34,7 +34,7 @@ SIDE_BY_SIDE_IN_RUNS = "p (c i j) -> p c j i"
 CHUNKS = [[0, 1], [2, 3], [4, 5], [6, 7], [8, 9], [10], [11]]
 LAST = len(CHUNKS) - 1
 TENSOR_CHUNKS = [2, 4, LAST]
-TENSOR_STARTS = {0: 2, 2: 4, 3: LAST}
+TENSOR_STARTS = {2: 4, 3: LAST}
 TENSOR_RETURNS = {2: [2], 4: [4, LAST]}
 
 LOADS = [
@@ -43,6 +43,7 @@ LOADS = [
 ]
 STORES = [(0, 4), (4, 2), (6, 2), (8, 1), (9, 1), (10, 1), (11, 1)]
 
+X3 = "x3"
 HI_PRODUCTS = [(HI, HI), (HI, LO)]
 LO_PRODUCTS = [(LO, HI)]
 ALL_PRODUCTS = HI_PRODUCTS + LO_PRODUCTS
@@ -114,7 +115,7 @@ def tile_mix_split3_fm_mul_kernel(tc, w, x, g, out):
             return w_span(c, 0, 1 if c in TENSOR_CHUNKS else len(CHUNKS[c]))
 
         def tensor_tile(c):
-            return w_span(c, len(CHUNKS[c]) - 1)
+            return x_span(3) if c == X3 else w_span(c, len(CHUNKS[c]) - 1)
 
         def raw(span):
             return span[0][:, :, span[1] : span[1] + span[2]]
@@ -215,11 +216,13 @@ def tile_mix_split3_fm_mul_kernel(tc, w, x, g, out):
             )
 
         sums = {}
+        passes = {}
 
         def multiply(c, a, products):
             t = CHUNKS[c][a]
             for w_part, x_part in products:
-                opens = (w_part, x_part) == ALL_PRODUCTS[0]
+                opens = t not in sums
+                passes[t] = passes.get(t, 0) + 1
                 if opens:
                     sums[t] = psum_sums.tile([P, T], F32, name="sums")
                 cols = slice(slot(c, a, w_part) * P, (slot(c, a, w_part) + 1) * P)
@@ -230,7 +233,7 @@ def tile_mix_split3_fm_mul_kernel(tc, w, x, g, out):
                     rhs=x_codes[:, x_part, :].bitcast(FP8X4),
                     rhs_scale=x_scales[:, x_part, :],
                     start=opens,
-                    stop=(w_part, x_part) == ALL_PRODUCTS[-1],
+                    stop=passes[t] == len(ALL_PRODUCTS),
                 )
 
         def quantize_and_multiply_tile(c, a):
@@ -259,35 +262,42 @@ def tile_mix_split3_fm_mul_kernel(tc, w, x, g, out):
             nc.vector.tensor_tensor(
                 out=in_runs(x_span(i)[4]), in0=rows_in_runs(raw(x_span(i))), in1=rows_in_runs(word_highs[i][:]), op=ALU.subtract
             )
-        for span in (x_span(2), x_span(3), paired(0)):
-            truncate(span)
-        prepare(2)
-        truncate(paired(1))
+        truncate(x_span(2))
+        mask_negated(X3)
+        subtract_on_tensor(X3)
+        high_from_negated(X3)
+        truncate(w_span(0, 0))
+        truncate(w_span(0, 1))
+        round_turned(X3)
         quantize_x(0, 2, HI)
         mask(x_span(2))
         quantize_x(0, 2, LO)
-        mask(x_span(3))
         subtract(x_span(2))
-        subtract(x_span(3))
-        mask_negated(TENSOR_STARTS[0])
-        subtract_on_tensor(TENSOR_STARTS[0])
-        high_from_negated(TENSOR_STARTS[0])
-        round_turned(TENSOR_STARTS[0])
         quantize_x(2, 2, HI)
-
-        mask(paired(0))
-        quantize_x(2, 2, LO)
+        mask_negated(2)
+        subtract_on_tensor(2)
+        turn_back([X3])
+        truncate(paired(1))
+        low_from_back(X3)
+        mask(w_span(0, 0))
+        mask(w_span(0, 1))
+        subtract(w_span(0, 0))
         quantize_slots(0, slot(0, 0, HI), 2)
         for a in range(2):
-            multiply(0, a, HI_PRODUCTS)
-        subtract(paired(0))
-        prepare(3)
-
+            multiply(0, a, [(HI, HI)])
+        subtract(w_span(0, 1))
+        prepare(2)
+        round_turned(2)
+        high_from_negated(2)
         mask(paired(1))
         quantize_slots(0, slot(0, 0, LO), 2)
-        subtract(paired(1))
         for a in range(2):
-            multiply(0, a, LO_PRODUCTS)
+            multiply(0, a, [(LO, HI)])
+        quantize_x(2, 2, LO)
+        for a in range(2):
+            multiply(0, a, [(HI, LO)])
+        subtract(paired(1))
+        prepare(3)
 
         for c in range(2, LAST):
             if c in TENSOR_STARTS:

@@ -31,19 +31,15 @@ RUN = 2
 ROWS_IN_RUNS = "p j (c i) -> p c j i"
 SIDE_BY_SIDE_IN_RUNS = "p (c i j) -> p c j i"
 
-CHUNKS = [[0, 1], [2, 3], [4, 5], [6, 7], [8, 9], [10], [11]]
-LAST = len(CHUNKS) - 1
-TENSOR_CHUNKS = [2, 4, LAST]
-TENSOR_STARTS = {2: 4, 3: LAST}
-TENSOR_RETURNS = {2: [2], 4: [4, LAST]}
+TILES = M // P
+X3 = "x3"
 
 LOADS = [
-    ("x", 0, 1), ("x", 1, 1), ("x", 2, 2), ("w", 0, 2), ("w", 4, 2), ("w", 2, 2), ("w", 6, 4),
+    ("x", 0, 1), ("x", 1, 1), ("x", 2, 2), ("w", 0, 2), ("w", 4, 1), ("w", 2, 2), ("w", 5, 5),
     ("g", 0, 2), ("w", 10, 2), ("g", 2, 2), ("g", 4, 4), ("g", 8, 4),
 ]
 STORES = [(0, 4), (4, 2), (6, 2), (8, 1), (9, 1), (10, 1), (11, 1)]
 
-X3 = "x3"
 HI_PRODUCTS = [(HI, HI), (HI, LO)]
 LO_PRODUCTS = [(LO, HI)]
 ALL_PRODUCTS = HI_PRODUCTS + LO_PRODUCTS
@@ -92,30 +88,29 @@ def tile_mix_split3_fm_mul_kernel(tc, w, x, g, out):
         x_parts = [sb.tile([P, T * PACK], BF16, name=f"x_parts{h}", align_bytes=MX_ALIGN) for h in (HI, LO)]
         x_codes = sb.tile([P, 2, T], U32, name="x_codes", align_bytes=MX_ALIGN)
         x_scales = sb.tile([P, 2, T], U8, name="x_scales", align_bytes=MX_ALIGN)
-        w_parts, w_codes, w_scales = [], [], []
-        for c, tiles in enumerate(CHUNKS):
-            slots = 2 * len(tiles)
-            w_parts.append(sb.tile([P, slots * slot_size], BF16, name=f"w_parts{c}", align_bytes=MX_ALIGN))
-            w_codes.append(sb.tile([P, slots * P], U32, name=f"w_codes{c}", align_bytes=MX_ALIGN))
-            w_scales.append(sb.tile([P, slots * P], U8, name=f"w_scales{c}", align_bytes=MX_ALIGN))
-
-        def slot(c, a, h):
-            return 2 * a + h if c in TENSOR_CHUNKS else h * len(CHUNKS[c]) + a
+        groups = [(t, t + 1) for t in range(0, TILES, 2)]
+        w_parts, w_codes, w_scales, slots = {}, {}, {}, {}
+        for tiles in groups:
+            count = 2 * len(tiles)
+            parts = sb.tile([P, count * slot_size], BF16, name=f"w_parts{tiles[0]}", align_bytes=MX_ALIGN)
+            codes = sb.tile([P, count * P], U32, name=f"w_codes{tiles[0]}", align_bytes=MX_ALIGN)
+            scales = sb.tile([P, count * P], U8, name=f"w_scales{tiles[0]}", align_bytes=MX_ALIGN)
+            for a, t in enumerate(tiles):
+                w_parts[t], w_codes[t], w_scales[t] = parts, codes, scales
+                for h in (HI, LO):
+                    slots[t, h] = h * len(tiles) + a
 
         def x_span(i):
             cols = slice(i * slot_size, (i + 1) * slot_size)
             return place["x", i] + (P, x_parts[HI][:, cols], x_parts[LO][:, cols])
 
-        def w_span(c, a, count=1):
-            high, low = slot(c, a, HI) * slot_size, slot(c, a, LO) * slot_size
+        def w_span(t, count=1):
+            high, low = slots[t, HI] * slot_size, slots[t, LO] * slot_size
             size = count * slot_size
-            return place["w", CHUNKS[c][a]] + (count * P, w_parts[c][:, high : high + size], w_parts[c][:, low : low + size])
+            return place["w", t] + (count * P, w_parts[t][:, high : high + size], w_parts[t][:, low : low + size])
 
-        def paired(c):
-            return w_span(c, 0, 1 if c in TENSOR_CHUNKS else len(CHUNKS[c]))
-
-        def tensor_tile(c):
-            return x_span(3) if c == X3 else w_span(c, len(CHUNKS[c]) - 1)
+        def span_of(t):
+            return x_span(3) if t == X3 else w_span(t)
 
         def raw(span):
             return span[0][:, :, span[1] : span[1] + span[2]]
@@ -140,38 +135,43 @@ def tile_mix_split3_fm_mul_kernel(tc, w, x, g, out):
 
         laid_out = {}
 
-        def prepare(c):
-            laid_out[c] = sb.tile([P, slot_size], F32, name=f"laid_out{c}", align_bytes=MX_ALIGN)
-            nc.scalar.copy(out=in_runs(laid_out[c][:]), in_=rows_in_runs(raw(w_span(c, 0))))
-            truncate(paired(c))
+        def lay_out(t):
+            laid_out[t] = sb.tile([P, slot_size], F32, name=f"laid_out{t}", align_bytes=MX_ALIGN)
+            nc.scalar.copy(out=in_runs(laid_out[t][:]), in_=rows_in_runs(raw(w_span(t))))
 
-        def subtract_on_gpsimd(c):
-            high, low = w_span(c, 0)[3:]
-            nc.gpsimd.tensor_tensor(out=low, in0=laid_out[c][:], in1=high, op=ALU.subtract)
+        def prepare(t, count=1):
+            lay_out(t)
+            truncate(w_span(t, count))
+
+        def subtract_on_gpsimd(t):
+            high, low = w_span(t)[3:]
+            nc.gpsimd.tensor_tensor(out=low, in0=laid_out[t][:], in1=high, op=ALU.subtract)
 
         negated = {}
         turned = {}
         rounded = {}
         back = {}
 
-        def mask_negated(c):
-            negated[c] = sb.tile([P, PACK, P], F32, name=f"negated{c}", align_bytes=MX_ALIGN)
+        def mask_negated(t, count=1):
+            stage, first = span_of(t)[:2]
+            words = sb.tile([P, PACK, count * P], F32, name=f"negated{t}", align_bytes=MX_ALIGN)
             nc.vector.tensor_scalar(
-                out=negated[c][:].bitcast(I32),
-                in0=raw(tensor_tile(c)).bitcast(I32),
+                out=words[:].bitcast(I32),
+                in0=stage[:, :, first : first + count * P].bitcast(I32),
                 scalar1=WORD_MASK,
                 scalar2=SIGN_BIT,
                 op0=ALU.bitwise_and,
                 op1=ALU.bitwise_xor,
             )
+            negated[t] = words[:]
 
-        def subtract_on_tensor(c):
-            turned[c] = psum_turned.tile([P, PACK, P], F32, name="turned")
-            terms = [raw(tensor_tile(c)), negated[c][:]]
+        def subtract_on_tensor(t):
+            turned[t] = psum_turned.tile([P, PACK, P], F32, name="turned")
+            terms = [raw(span_of(t)), negated[t]]
             for s, rows in enumerate(terms):
                 for j in range(PACK):
                     nc.tensor.matmul(
-                        turned[c][:, j, :],
+                        turned[t][:, j, :],
                         lhsT=rows[:, j, :],
                         rhs=identity[:],
                         is_transpose=True,
@@ -179,29 +179,29 @@ def tile_mix_split3_fm_mul_kernel(tc, w, x, g, out):
                         stop=s == len(terms) - 1 and j == PACK - 1,
                     )
 
-        def round_turned(c):
-            rounded[c] = sb.tile([P, slot_size], BF16, name=f"rounded{c}", align_bytes=MX_ALIGN)
+        def round_turned(t):
+            rounded[t] = sb.tile([P, slot_size], BF16, name=f"rounded{t}", align_bytes=MX_ALIGN)
             nc.scalar.copy(
-                out=rounded[c][:].rearrange("n (u p e) -> n u p e", u=2, e=2),
-                in_=turned[c][:].rearrange("n (u e) p -> n u p e", e=2),
+                out=rounded[t][:].rearrange("n (u p e) -> n u p e", u=2, e=2),
+                in_=turned[t][:].rearrange("n (u e) p -> n u p e", e=2),
             )
 
-        def turn_back(chunks):
+        def turn_back(*tiles):
             bank = psum_back.tile([P, 2, 2, P], F32, name="back")
-            for a, c in enumerate(chunks):
-                words = rounded[c][:].bitcast(F32)
+            for a, t in enumerate(tiles):
+                words = rounded[t][:].bitcast(F32)
                 for u in range(2):
                     nc.tensor.transpose(bank[:, a, u, :], words[:, u * P : (u + 1) * P], identity[:])
-                back[c] = bank[:, a, :, :]
+                back[t] = bank[:, a, :, :]
 
-        def low_from_back(c):
+        def low_from_back(t):
             nc.scalar.copy(
-                out=tensor_tile(c)[4].bitcast(F32).rearrange("p (n u) -> p n u", u=2),
-                in_=back[c].rearrange("p u n -> p n u"),
+                out=span_of(t)[4].bitcast(F32).rearrange("p (n u) -> p n u", u=2),
+                in_=back[t].rearrange("p u n -> p n u"),
             )
 
-        def high_from_negated(c):
-            nc.scalar.activation(out=in_runs(tensor_tile(c)[3]), in_=rows_in_runs(negated[c][:]), func=ACT.Copy, scale=-1.0)
+        def high_from_negated(t):
+            nc.scalar.activation(out=in_runs(span_of(t)[3]), in_=rows_in_runs(negated[t]), func=ACT.Copy, scale=-1.0)
 
         def quantize_x(first, count, h):
             t0, t1 = first * P, (first + count) * P
@@ -209,41 +209,44 @@ def tile_mix_split3_fm_mul_kernel(tc, w, x, g, out):
                 out=x_codes[:, h, t0:t1].bitcast(FP8X4), scales=x_scales[:, h, t0:t1], in_=x_parts[h][:, t0 * PACK : t1 * PACK]
             )
 
-        def quantize_slots(c, first, count):
-            n0, n1 = first * P, (first + count) * P
+        def quantize_slots(t, h, count):
+            n0, n1 = slots[t, h] * P, (slots[t, h] + count) * P
             nc.vector.quantize_mx(
-                out=w_codes[c][:, n0:n1].bitcast(FP8X4), scales=w_scales[c][:, n0:n1], in_=w_parts[c][:, n0 * PACK : n1 * PACK]
+                out=w_codes[t][:, n0:n1].bitcast(FP8X4), scales=w_scales[t][:, n0:n1], in_=w_parts[t][:, n0 * PACK : n1 * PACK]
             )
 
         sums = {}
         passes = {}
 
-        def multiply(c, a, products):
-            t = CHUNKS[c][a]
+        def multiply(t, products):
             for w_part, x_part in products:
                 opens = t not in sums
                 passes[t] = passes.get(t, 0) + 1
                 if opens:
                     sums[t] = psum_sums.tile([P, T], F32, name="sums")
-                cols = slice(slot(c, a, w_part) * P, (slot(c, a, w_part) + 1) * P)
+                cols = slice(slots[t, w_part] * P, (slots[t, w_part] + 1) * P)
                 nc.tensor.matmul_mx(
                     out=sums[t][:],
-                    lhsT=w_codes[c][:, cols].bitcast(FP8X4),
-                    lhsT_scale=w_scales[c][:, cols],
+                    lhsT=w_codes[t][:, cols].bitcast(FP8X4),
+                    lhsT_scale=w_scales[t][:, cols],
                     rhs=x_codes[:, x_part, :].bitcast(FP8X4),
                     rhs_scale=x_scales[:, x_part, :],
                     start=opens,
                     stop=passes[t] == len(ALL_PRODUCTS),
                 )
 
-        def quantize_and_multiply_tile(c, a):
-            quantize_slots(c, slot(c, a, HI), 2)
-            multiply(c, a, ALL_PRODUCTS)
+        def multiply_pair(t, products):
+            for a in range(2):
+                multiply(t + a, products)
+
+        def quantize_and_multiply(t):
+            quantize_slots(t, HI, 4)
+            multiply_pair(t, ALL_PRODUCTS)
 
         read = set()
 
-        def read_out(c):
-            for t in reversed(CHUNKS[c]) if c in TENSOR_CHUNKS else CHUNKS[c]:
+        def read_out(*tiles):
+            for t in tiles:
                 first, count, stage = results[t]
                 nc.vector.tensor_tensor(out=stage[:, t - first, :], in0=sums[t][:], in1=g_sb[t], op=ALU.mult)
                 read.add(t)
@@ -266,72 +269,72 @@ def tile_mix_split3_fm_mul_kernel(tc, w, x, g, out):
         mask_negated(X3)
         subtract_on_tensor(X3)
         high_from_negated(X3)
-        truncate(w_span(0, 0))
-        truncate(w_span(0, 1))
+        truncate(w_span(0))
+        truncate(w_span(1))
         round_turned(X3)
         quantize_x(0, 2, HI)
         mask(x_span(2))
         quantize_x(0, 2, LO)
         subtract(x_span(2))
         quantize_x(2, 2, HI)
-        mask_negated(2)
-        subtract_on_tensor(2)
-        turn_back([X3])
-        truncate(paired(1))
+        mask_negated(4)
+        subtract_on_tensor(4)
+        turn_back(X3)
+        truncate(w_span(2, 2))
         low_from_back(X3)
-        mask(w_span(0, 0))
-        mask(w_span(0, 1))
-        subtract(w_span(0, 0))
-        quantize_slots(0, slot(0, 0, HI), 2)
-        for a in range(2):
-            multiply(0, a, [(HI, HI)])
-        subtract(w_span(0, 1))
-        prepare(2)
-        round_turned(2)
-        high_from_negated(2)
-        mask(paired(1))
-        quantize_slots(0, slot(0, 0, LO), 2)
-        for a in range(2):
-            multiply(0, a, [(LO, HI)])
+        mask(w_span(0))
+        mask(w_span(1))
+        subtract(w_span(0))
+        quantize_slots(0, HI, 2)
+        multiply_pair(0, [(HI, HI)])
+        subtract(w_span(1))
+        round_turned(4)
+        prepare(5)
+        high_from_negated(4)
+        mask(w_span(2, 2))
+        quantize_slots(0, LO, 2)
+        multiply_pair(0, [(LO, HI)])
         quantize_x(2, 2, LO)
-        for a in range(2):
-            multiply(0, a, [(HI, LO)])
-        subtract(paired(1))
-        prepare(3)
-
-        for c in range(2, LAST):
-            if c in TENSOR_STARTS:
-                mask_negated(TENSOR_STARTS[c])
-            if c in TENSOR_RETURNS:
-                turn_back(TENSOR_RETURNS[c])
-                for returning in TENSOR_RETURNS[c]:
-                    low_from_back(returning)
-            if c + 1 in TENSOR_CHUNKS:
-                high_from_negated(c + 1)
-            if c in TENSOR_STARTS:
-                subtract_on_tensor(TENSOR_STARTS[c])
-                round_turned(TENSOR_STARTS[c])
-            if c + 2 < LAST:
-                prepare(c + 2)
-            if c - 1 in TENSOR_CHUNKS:
-                quantize_and_multiply_tile(c - 1, 1)
-            mask(paired(c))
-            subtract_on_gpsimd(c)
-            if c - 1 in TENSOR_CHUNKS:
-                quantize_and_multiply_tile(c - 1, 0)
-            else:
-                quantize_slots(c - 1, 0, 4)
-                for a in range(2):
-                    multiply(c - 1, a, ALL_PRODUCTS)
-            read_out(c - 2)
-            if len(CHUNKS[c]) == 2 and c not in TENSOR_CHUNKS:
-                subtract(w_span(c, 1))
-
-        for c in (LAST, LAST - 1):
-            quantize_and_multiply_tile(c, 0)
-        for c in (LAST - 2, LAST):
-            read_out(c)
-        t = CHUNKS[LAST - 1][0]
+        multiply_pair(0, [(HI, LO)])
+        subtract(w_span(2, 2))
+        prepare(6, 2)
+        mask_negated(9)
+        turn_back(4)
+        subtract_on_tensor(9)
+        low_from_back(4)
+        round_turned(9)
+        prepare(8)
+        mask(w_span(5))
+        subtract_on_gpsimd(5)
+        quantize_and_multiply(2)
+        read_out(0, 1)
+        mask_negated(11)
+        subtract_on_tensor(11)
+        high_from_negated(9)
+        round_turned(11)
+        prepare(10)
+        mask(w_span(6, 2))
+        subtract_on_gpsimd(6)
+        quantize_and_multiply(4)
+        read_out(2, 3)
+        subtract(w_span(7))
+        turn_back(9, 11)
+        low_from_back(9)
+        high_from_negated(11)
+        low_from_back(11)
+        mask(w_span(8))
+        subtract_on_gpsimd(8)
+        quantize_and_multiply(6)
+        read_out(4, 5)
+        mask(w_span(10))
+        subtract_on_gpsimd(10)
+        quantize_and_multiply(8)
+        read_out(6, 7)
+        quantize_slots(10, HI, 2)
+        quantize_slots(10, LO, 2)
+        multiply_pair(10, ALL_PRODUCTS)
+        read_out(8, 9, 10)
+        t = TILES - 1
         stage = results[t][2]
         for half in (slice(0, T // 2), slice(T // 2, T)):
             nc.vector.tensor_tensor(out=stage[:, 0, half], in0=sums[t][:, half], in1=g_sb[t][:, half], op=ALU.mult)

@@ -35,8 +35,7 @@ TILES = M // P
 X3 = "x3"
 
 LOADS = [
-    ("x", 0, 1), ("x", 1, 1), ("x", 2, 2), ("w", 0, 2), ("w", 4, 1), ("w", 2, 2), ("w", 5, 5),
-    ("g", 0, 2), ("w", 10, 2), ("g", 2, 2), ("g", 4, 4), ("g", 8, 4),
+    ("x", 0, 1), ("x", 1, 1), ("x", 2, 2), ("w", 0, 2), ("w", 4, 1), ("w", 2, 2), ("w", 5, 1), ("w", 6, 4), ("g", 0, 2), ("w", 10, 2), ("g", 2, 2), ("g", 4, 4), ("g", 8, 4),
 ]
 STORES = [(0, 4), (4, 2), (6, 2), (8, 1), (9, 1), (10, 1), (11, 1)]
 

@@ -28,6 +28,7 @@ PAIR_MASK = 0xFFF0FFF0 - (1 << 32)
 SIGN_BIT = -(1 << 31)
 
 RUN = 2
+LINE = 4
 ROWS_IN_RUNS = "p j (c i) -> p c j i"
 SIDE_BY_SIDE_IN_RUNS = "p (c i j) -> p c j i"
 
@@ -35,9 +36,11 @@ TILES = M // P
 X3 = "x3"
 
 LOADS = [
-    ("x", 0, 1), ("x", 1, 1), ("x", 2, 2), ("w", 0, 2), ("w", 4, 1), ("w", 2, 2), ("w", 5, 1), ("w", 6, 4), ("g", 0, 2), ("w", 10, 2), ("g", 2, 2), ("g", 4, 4), ("g", 8, 4),
+    ("x", range(0, 1)), ("x", range(1, 2)), ("x", range(2, 4)), ("w", range(0, 2)), ("w", range(2, 4)), ("w", range(4, 6)),
+    ("w", range(6, 10)), ("g", range(0, 2)), ("w", range(10, 12)), ("g", range(3, 5)), ("g", range(2, 6, 3)), ("g", range(6, 12)),
 ]
-STORES = [(0, 4), (4, 2), (6, 2), (8, 1), (9, 1), (10, 1), (11, 1)]
+STORES = [range(0, 2), range(3, 5), range(2, 6, 3), range(6, 8), range(8, 9), range(9, 10), range(10, 11), range(11, 12)]
+GROUPS = [(0, 1), (3, 4), (2, 5), (6, 7), (8, 9), (10, 11)]
 
 HI_PRODUCTS = [(HI, HI), (HI, LO)]
 LO_PRODUCTS = [(LO, HI)]
@@ -66,30 +69,30 @@ def tile_mix_split3_fm_mul_kernel(tc, w, x, g, out):
         out_tiles = out.rearrange("(a p) t -> p a t", p=P)
         place = {}
         g_sb = {}
-        for operand, first, count in LOADS:
+        for operand, tiles in LOADS:
+            first, count = tiles.start, len(tiles)
             if operand == "g":
                 stage = sb.tile([P, count, T], F32, name=f"g_sb{first}", align_bytes=DMA_ALIGN)
-                nc.sync.dma_start(out=stage[:], in_=g_tiles[:, first : first + count, :])
-                for a in range(count):
-                    g_sb[first + a] = stage[:, a, :]
+                nc.sync.dma_start(out=stage[:], in_=g_tiles[:, first : tiles[-1] + 1 : tiles.step, :])
+                for a, t in enumerate(tiles):
+                    g_sb[t] = stage[:, a, :]
             else:
                 stage = sb.tile([P, PACK, count * P], F32, name=f"{operand}_raw{first}", align_bytes=DMA_ALIGN)
                 nc.sync.dma_start(out=stage[:], in_=k_rows[operand][:, :, first * P : (first + count) * P])
                 for a in range(count):
                     place[operand, first + a] = (stage, a * P)
         results = {}
-        for first, count in STORES:
-            stage = sb.tile([P, count, T], F32, name=f"result{first}", align_bytes=DMA_ALIGN)
-            for a in range(count):
-                results[first + a] = (first, count, stage)
+        for tiles in STORES:
+            stage = sb.tile([P, len(tiles), T], F32, name=f"result{tiles.start}", align_bytes=DMA_ALIGN)
+            for t in tiles:
+                results[t] = (tiles, stage)
 
         slot_size = P * PACK
         x_parts = [sb.tile([P, T * PACK], BF16, name=f"x_parts{h}", align_bytes=MX_ALIGN) for h in (HI, LO)]
         x_codes = sb.tile([P, 2, T], U32, name="x_codes", align_bytes=MX_ALIGN)
         x_scales = sb.tile([P, 2, T], U8, name="x_scales", align_bytes=MX_ALIGN)
-        groups = [(t, t + 1) for t in range(0, TILES, 2)]
         w_parts, w_codes, w_scales, slots = {}, {}, {}, {}
-        for tiles in groups:
+        for tiles in GROUPS:
             count = 2 * len(tiles)
             parts = sb.tile([P, count * slot_size], BF16, name=f"w_parts{tiles[0]}", align_bytes=MX_ALIGN)
             codes = sb.tile([P, count * P], U32, name=f"w_codes{tiles[0]}", align_bytes=MX_ALIGN)
@@ -114,16 +117,16 @@ def tile_mix_split3_fm_mul_kernel(tc, w, x, g, out):
         def raw(span):
             return span[0][:, :, span[1] : span[1] + span[2]]
 
-        def rows_in_runs(rows):
-            return rows.rearrange(ROWS_IN_RUNS, i=RUN)
+        def rows_in_runs(rows, run=RUN):
+            return rows.rearrange(ROWS_IN_RUNS, i=run)
 
-        def in_runs(part):
-            return part.rearrange(SIDE_BY_SIDE_IN_RUNS, i=RUN, j=PACK)
+        def in_runs(part, run=RUN):
+            return part.rearrange(SIDE_BY_SIDE_IN_RUNS, i=run, j=PACK)
 
         def truncate(span):
             stage, first, width, high = span[:4]
-            halves = stage[:].bitcast(BF16).rearrange("p j (c i h) -> p c j i h", i=RUN, h=2)
-            nc.scalar.copy(out=in_runs(high), in_=halves[:, first // RUN : (first + width) // RUN, :, :, 1])
+            halves = stage[:].bitcast(BF16).rearrange("p j (c i h) -> p c j i h", i=LINE, h=2)
+            nc.scalar.copy(out=in_runs(high, LINE), in_=halves[:, first // LINE : (first + width) // LINE, :, :, 1])
 
         def mask(span):
             words = span[3].bitcast(I32)
@@ -200,7 +203,7 @@ def tile_mix_split3_fm_mul_kernel(tc, w, x, g, out):
             )
 
         def high_from_negated(t):
-            nc.scalar.activation(out=in_runs(span_of(t)[3]), in_=rows_in_runs(negated[t]), func=ACT.Copy, scale=-1.0)
+            nc.scalar.activation(out=in_runs(span_of(t)[3], LINE), in_=rows_in_runs(negated[t], LINE), func=ACT.Copy, scale=-1.0)
 
         def quantize_x(first, count, h):
             t0, t1 = first * P, (first + count) * P
@@ -235,8 +238,8 @@ def tile_mix_split3_fm_mul_kernel(tc, w, x, g, out):
                 )
 
         def multiply_pair(t, products):
-            for a in range(2):
-                multiply(t + a, products)
+            for u in [tiles for tiles in GROUPS if tiles[0] == t][0]:
+                multiply(u, products)
 
         def quantize_and_multiply(t):
             quantize_slots(t, HI, 4)
@@ -246,11 +249,11 @@ def tile_mix_split3_fm_mul_kernel(tc, w, x, g, out):
 
         def read_out(*tiles):
             for t in tiles:
-                first, count, stage = results[t]
-                nc.vector.tensor_tensor(out=stage[:, t - first, :], in0=sums[t][:], in1=g_sb[t], op=ALU.mult)
+                together, stage = results[t]
+                nc.vector.tensor_tensor(out=stage[:, together.index(t), :], in0=sums[t][:], in1=g_sb[t], op=ALU.mult)
                 read.add(t)
-                if all(first + a in read for a in range(count)):
-                    nc.sync.dma_start(out=out_tiles[:, first : first + count, :], in_=stage[:])
+                if all(u in read for u in together):
+                    nc.sync.dma_start(out=out_tiles[:, together.start : together[-1] + 1 : together.step, :], in_=stage[:])
 
         word_highs = []
         for i in range(2):
@@ -258,7 +261,7 @@ def tile_mix_split3_fm_mul_kernel(tc, w, x, g, out):
             nc.vector.tensor_scalar(
                 out=words[:].bitcast(I32), in0=raw(x_span(i)).bitcast(I32), scalar1=WORD_MASK, scalar2=None, op0=ALU.bitwise_and
             )
-            nc.scalar.copy(out=in_runs(x_span(i)[3]), in_=rows_in_runs(words[:]))
+            nc.scalar.copy(out=in_runs(x_span(i)[3], LINE), in_=rows_in_runs(words[:], LINE))
             word_highs.append(words)
         for i in range(2):
             nc.vector.tensor_tensor(
@@ -276,10 +279,11 @@ def tile_mix_split3_fm_mul_kernel(tc, w, x, g, out):
         quantize_x(0, 2, LO)
         subtract(x_span(2))
         quantize_x(2, 2, HI)
-        mask_negated(4)
-        subtract_on_tensor(4)
+        mask_negated(2)
+        subtract_on_tensor(2)
         turn_back(X3)
-        truncate(w_span(2, 2))
+        truncate(w_span(3))
+        truncate(w_span(4))
         low_from_back(X3)
         mask(w_span(0))
         mask(w_span(1))
@@ -287,25 +291,26 @@ def tile_mix_split3_fm_mul_kernel(tc, w, x, g, out):
         quantize_slots(0, HI, 2)
         multiply_pair(0, [(HI, HI)])
         subtract(w_span(1))
-        round_turned(4)
+        round_turned(2)
         prepare(5)
-        high_from_negated(4)
-        mask(w_span(2, 2))
+        high_from_negated(2)
+        mask(w_span(3, 2))
         quantize_slots(0, LO, 2)
         multiply_pair(0, [(LO, HI)])
         quantize_x(2, 2, LO)
         multiply_pair(0, [(HI, LO)])
-        subtract(w_span(2, 2))
+        subtract(w_span(3))
+        subtract(w_span(4))
         prepare(6, 2)
         mask_negated(9)
-        turn_back(4)
+        turn_back(2)
         subtract_on_tensor(9)
-        low_from_back(4)
+        low_from_back(2)
         round_turned(9)
         prepare(8)
         mask(w_span(5))
         subtract_on_gpsimd(5)
-        quantize_and_multiply(2)
+        quantize_and_multiply(3)
         read_out(0, 1)
         mask_negated(11)
         subtract_on_tensor(11)
@@ -314,8 +319,8 @@ def tile_mix_split3_fm_mul_kernel(tc, w, x, g, out):
         prepare(10)
         mask(w_span(6, 2))
         subtract_on_gpsimd(6)
-        quantize_and_multiply(4)
-        read_out(2, 3)
+        quantize_and_multiply(2)
+        read_out(3, 4)
         subtract(w_span(7))
         turn_back(9, 11)
         low_from_back(9)
@@ -324,7 +329,7 @@ def tile_mix_split3_fm_mul_kernel(tc, w, x, g, out):
         mask(w_span(8))
         subtract_on_gpsimd(8)
         quantize_and_multiply(6)
-        read_out(4, 5)
+        read_out(2, 5)
         mask(w_span(10))
         subtract_on_gpsimd(10)
         quantize_and_multiply(8)
@@ -334,7 +339,7 @@ def tile_mix_split3_fm_mul_kernel(tc, w, x, g, out):
         multiply_pair(10, ALL_PRODUCTS)
         read_out(8, 9, 10)
         t = TILES - 1
-        stage = results[t][2]
+        stage = results[t][1]
         for half in (slice(0, T // 2), slice(T // 2, T)):
             nc.vector.tensor_tensor(out=stage[:, 0, half], in0=sums[t][:, half], in1=g_sb[t][:, half], op=ALU.mult)
             nc.sync.dma_start(out=out_tiles[:, t, half], in_=stage[:, 0, half])

@@ -19,7 +19,7 @@ P = 128
 PACK = 4
 HI, LO = 0, 1
 MX_ALIGN = 64
-DMA_ALIGN = 256
+DMA_ALIGN = 2048
 
 SUM_BANKS, TURNED_BANKS, BACK_BANKS = 5, 2, 1
 
@@ -27,24 +27,24 @@ WORD_MASK = 0xFFF00000 - (1 << 32)
 PAIR_MASK = 0xFFF0FFF0 - (1 << 32)
 SIGN_BIT = -(1 << 31)
 
-RUN = 2
-LINE = 4
+PAIR_RUN, LINE_RUN = 2, 4
 ROWS_IN_RUNS = "p j (c i) -> p c j i"
 SIDE_BY_SIDE_IN_RUNS = "p (c i j) -> p c j i"
 
-TILES = M // P
-X3 = "x3"
+CHUNKS = [(0, 1), (3, 4), (2, 5), (6, 7), (8, 9), (10, 11)]
+LAST = len(CHUNKS) - 1
+GPSIMD_TILE = {2: 5, 3: 6, 4: 8, 5: 10}
+LAST_PIECE = "last piece of x"
+EARLY_TILE, MIDDLE_TILE, LAST_TILE = 2, 9, 11
+VECTOR_TILE = 7
 
 LOADS = [
     ("x", range(0, 1)), ("x", range(1, 2)), ("x", range(2, 4)), ("w", range(0, 2)), ("w", range(2, 4)), ("w", range(4, 6)),
     ("w", range(6, 10)), ("g", range(0, 2)), ("w", range(10, 12)), ("g", range(3, 5)), ("g", range(2, 6, 3)), ("g", range(6, 12)),
 ]
-STORES = [range(0, 2), range(3, 5), range(2, 6, 3), range(6, 8), range(8, 9), range(9, 10), range(10, 11), range(11, 12)]
-GROUPS = [(0, 1), (3, 4), (2, 5), (6, 7), (8, 9), (10, 11)]
+STORES = [range(0, 2), range(3, 5), range(2, 6, 3), range(6, 8)] + [range(t, t + 1) for t in range(8, 12)]
 
-HI_PRODUCTS = [(HI, HI), (HI, LO)]
-LO_PRODUCTS = [(LO, HI)]
-ALL_PRODUCTS = HI_PRODUCTS + LO_PRODUCTS
+PRODUCTS = [(HI, HI), (HI, LO), (LO, HI)]
 
 
 def tile_mix_split3_fm_mul_kernel(tc, w, x, g, out):
@@ -55,14 +55,6 @@ def tile_mix_split3_fm_mul_kernel(tc, w, x, g, out):
         psum_turned = ctx.enter_context(tc.psum_pool(name="psum_turned", bufs=TURNED_BANKS))
         psum_back = ctx.enter_context(tc.psum_pool(name="psum_back", bufs=BACK_BANKS))
         ctx.enter_context(tc.manual_schedule())
-
-        warm_in = sb.tile([P, 2], BF16, name="warm_in")
-        warm_out = sb.tile([P, 2], BF16, name="warm_out")
-        nc.vector.memset(warm_in[:], 0.0)
-        nc.scalar.copy(out=warm_out[:], in_=warm_in[:])
-
-        identity = sb.tile([P, P], F32, name="identity", align_bytes=MX_ALIGN)
-        make_identity(nc, identity[:])
 
         k_rows = {"x": x.rearrange("(p j) t -> p j t", j=PACK), "w": w.rearrange("(p j) n -> p j n", j=PACK)}
         g_tiles = g.rearrange("(a p) t -> p a t", p=P)
@@ -87,12 +79,15 @@ def tile_mix_split3_fm_mul_kernel(tc, w, x, g, out):
             for t in tiles:
                 results[t] = (tiles, stage)
 
+        identity = sb.tile([P, P], F32, name="identity", align_bytes=MX_ALIGN)
+        make_identity(nc, identity[:])
+
         slot_size = P * PACK
         x_parts = [sb.tile([P, T * PACK], BF16, name=f"x_parts{h}", align_bytes=MX_ALIGN) for h in (HI, LO)]
         x_codes = sb.tile([P, 2, T], U32, name="x_codes", align_bytes=MX_ALIGN)
         x_scales = sb.tile([P, 2, T], U8, name="x_scales", align_bytes=MX_ALIGN)
         w_parts, w_codes, w_scales, slots = {}, {}, {}, {}
-        for tiles in GROUPS:
+        for tiles in CHUNKS:
             count = 2 * len(tiles)
             parts = sb.tile([P, count * slot_size], BF16, name=f"w_parts{tiles[0]}", align_bytes=MX_ALIGN)
             codes = sb.tile([P, count * P], U32, name=f"w_codes{tiles[0]}", align_bytes=MX_ALIGN)
@@ -112,21 +107,21 @@ def tile_mix_split3_fm_mul_kernel(tc, w, x, g, out):
             return place["w", t] + (count * P, w_parts[t][:, high : high + size], w_parts[t][:, low : low + size])
 
         def span_of(t):
-            return x_span(3) if t == X3 else w_span(t)
+            return x_span(T // P - 1) if t == LAST_PIECE else w_span(t)
 
         def raw(span):
             return span[0][:, :, span[1] : span[1] + span[2]]
 
-        def rows_in_runs(rows, run=RUN):
+        def rows_in_runs(rows, run=PAIR_RUN):
             return rows.rearrange(ROWS_IN_RUNS, i=run)
 
-        def in_runs(part, run=RUN):
+        def in_runs(part, run=PAIR_RUN):
             return part.rearrange(SIDE_BY_SIDE_IN_RUNS, i=run, j=PACK)
 
         def truncate(span):
             stage, first, width, high = span[:4]
-            halves = stage[:].bitcast(BF16).rearrange("p j (c i h) -> p c j i h", i=LINE, h=2)
-            nc.scalar.copy(out=in_runs(high, LINE), in_=halves[:, first // LINE : (first + width) // LINE, :, :, 1])
+            halves = stage[:].bitcast(BF16).rearrange("p j (c i h) -> p c j i h", i=LINE_RUN, h=2)
+            nc.scalar.copy(out=in_runs(high, LINE_RUN), in_=halves[:, first // LINE_RUN : (first + width) // LINE_RUN, :, :, 1])
 
         def mask(span):
             words = span[3].bitcast(I32)
@@ -137,12 +132,9 @@ def tile_mix_split3_fm_mul_kernel(tc, w, x, g, out):
 
         laid_out = {}
 
-        def lay_out(t):
+        def prepare(t, count=1):
             laid_out[t] = sb.tile([P, slot_size], F32, name=f"laid_out{t}", align_bytes=MX_ALIGN)
             nc.scalar.copy(out=in_runs(laid_out[t][:]), in_=rows_in_runs(raw(w_span(t))))
-
-        def prepare(t, count=1):
-            lay_out(t)
             truncate(w_span(t, count))
 
         def subtract_on_gpsimd(t):
@@ -154,22 +146,20 @@ def tile_mix_split3_fm_mul_kernel(tc, w, x, g, out):
         rounded = {}
         back = {}
 
-        def mask_negated(t, count=1):
-            stage, first = span_of(t)[:2]
-            words = sb.tile([P, PACK, count * P], F32, name=f"negated{t}", align_bytes=MX_ALIGN)
+        def mask_negated(t):
+            negated[t] = sb.tile([P, PACK, P], F32, name=f"negated{len(negated)}", align_bytes=MX_ALIGN)
             nc.vector.tensor_scalar(
-                out=words[:].bitcast(I32),
-                in0=stage[:, :, first : first + count * P].bitcast(I32),
+                out=negated[t][:].bitcast(I32),
+                in0=raw(span_of(t)).bitcast(I32),
                 scalar1=WORD_MASK,
                 scalar2=SIGN_BIT,
                 op0=ALU.bitwise_and,
                 op1=ALU.bitwise_xor,
             )
-            negated[t] = words[:]
 
         def subtract_on_tensor(t):
             turned[t] = psum_turned.tile([P, PACK, P], F32, name="turned")
-            terms = [raw(span_of(t)), negated[t]]
+            terms = [raw(span_of(t)), negated[t][:]]
             for s, rows in enumerate(terms):
                 for j in range(PACK):
                     nc.tensor.matmul(
@@ -182,7 +172,7 @@ def tile_mix_split3_fm_mul_kernel(tc, w, x, g, out):
                     )
 
         def round_turned(t):
-            rounded[t] = sb.tile([P, slot_size], BF16, name=f"rounded{t}", align_bytes=MX_ALIGN)
+            rounded[t] = sb.tile([P, slot_size], BF16, name=f"rounded{len(rounded)}", align_bytes=MX_ALIGN)
             nc.scalar.copy(
                 out=rounded[t][:].rearrange("n (u p e) -> n u p e", u=2, e=2),
                 in_=turned[t][:].rearrange("n (u e) p -> n u p e", e=2),
@@ -203,7 +193,7 @@ def tile_mix_split3_fm_mul_kernel(tc, w, x, g, out):
             )
 
         def high_from_negated(t):
-            nc.scalar.activation(out=in_runs(span_of(t)[3], LINE), in_=rows_in_runs(negated[t], LINE), func=ACT.Copy, scale=-1.0)
+            nc.scalar.activation(out=in_runs(span_of(t)[3], LINE_RUN), in_=rows_in_runs(negated[t][:], LINE_RUN), func=ACT.Copy, scale=-1.0)
 
         def quantize_x(first, count, h):
             t0, t1 = first * P, (first + count) * P
@@ -211,8 +201,9 @@ def tile_mix_split3_fm_mul_kernel(tc, w, x, g, out):
                 out=x_codes[:, h, t0:t1].bitcast(FP8X4), scales=x_scales[:, h, t0:t1], in_=x_parts[h][:, t0 * PACK : t1 * PACK]
             )
 
-        def quantize_slots(t, h, count):
-            n0, n1 = slots[t, h] * P, (slots[t, h] + count) * P
+        def quantize_chunk(c, parts):
+            t = CHUNKS[c][0]
+            n0, n1 = slots[t, parts[0]] * P, (slots[t, parts[-1]] + len(CHUNKS[c])) * P
             nc.vector.quantize_mx(
                 out=w_codes[t][:, n0:n1].bitcast(FP8X4), scales=w_scales[t][:, n0:n1], in_=w_parts[t][:, n0 * PACK : n1 * PACK]
             )
@@ -220,30 +211,22 @@ def tile_mix_split3_fm_mul_kernel(tc, w, x, g, out):
         sums = {}
         passes = {}
 
-        def multiply(t, products):
-            for w_part, x_part in products:
-                opens = t not in sums
-                passes[t] = passes.get(t, 0) + 1
-                if opens:
-                    sums[t] = psum_sums.tile([P, T], F32, name="sums")
-                cols = slice(slots[t, w_part] * P, (slots[t, w_part] + 1) * P)
-                nc.tensor.matmul_mx(
-                    out=sums[t][:],
-                    lhsT=w_codes[t][:, cols].bitcast(FP8X4),
-                    lhsT_scale=w_scales[t][:, cols],
-                    rhs=x_codes[:, x_part, :].bitcast(FP8X4),
-                    rhs_scale=x_scales[:, x_part, :],
-                    start=opens,
-                    stop=passes[t] == len(ALL_PRODUCTS),
-                )
-
-        def multiply_pair(t, products):
-            for u in [tiles for tiles in GROUPS if tiles[0] == t][0]:
-                multiply(u, products)
-
-        def quantize_and_multiply(t):
-            quantize_slots(t, HI, 4)
-            multiply_pair(t, ALL_PRODUCTS)
+        def multiply(c, products):
+            for t in CHUNKS[c]:
+                for w_part, x_part in products:
+                    passes[t] = passes.get(t, 0) + 1
+                    if passes[t] == 1:
+                        sums[t] = psum_sums.tile([P, T], F32, name="sums")
+                    cols = slice(slots[t, w_part] * P, (slots[t, w_part] + 1) * P)
+                    nc.tensor.matmul_mx(
+                        out=sums[t][:],
+                        lhsT=w_codes[t][:, cols].bitcast(FP8X4),
+                        lhsT_scale=w_scales[t][:, cols],
+                        rhs=x_codes[:, x_part, :].bitcast(FP8X4),
+                        rhs_scale=x_scales[:, x_part, :],
+                        start=passes[t] == 1,
+                        stop=passes[t] == len(PRODUCTS),
+                    )
 
         read = set()
 
@@ -255,91 +238,94 @@ def tile_mix_split3_fm_mul_kernel(tc, w, x, g, out):
                 if all(u in read for u in together):
                     nc.sync.dma_start(out=out_tiles[:, together.start : together[-1] + 1 : together.step, :], in_=stage[:])
 
+        def step(c, masked=1):
+            mask(w_span(GPSIMD_TILE[c], masked))
+            subtract_on_gpsimd(GPSIMD_TILE[c])
+            quantize_chunk(c - 1, (HI, LO))
+            multiply(c - 1, PRODUCTS)
+            read_out(*CHUNKS[c - 2])
+
         word_highs = []
         for i in range(2):
             words = sb.tile([P, PACK, P], F32, name=f"word_high{i}", align_bytes=MX_ALIGN)
             nc.vector.tensor_scalar(
                 out=words[:].bitcast(I32), in0=raw(x_span(i)).bitcast(I32), scalar1=WORD_MASK, scalar2=None, op0=ALU.bitwise_and
             )
-            nc.scalar.copy(out=in_runs(x_span(i)[3], LINE), in_=rows_in_runs(words[:], LINE))
+            nc.scalar.copy(out=in_runs(x_span(i)[3], LINE_RUN), in_=rows_in_runs(words[:], LINE_RUN))
             word_highs.append(words)
         for i in range(2):
             nc.vector.tensor_tensor(
                 out=in_runs(x_span(i)[4]), in0=rows_in_runs(raw(x_span(i))), in1=rows_in_runs(word_highs[i][:]), op=ALU.subtract
             )
+
         truncate(x_span(2))
-        mask_negated(X3)
-        subtract_on_tensor(X3)
-        high_from_negated(X3)
-        truncate(w_span(0))
-        truncate(w_span(1))
-        round_turned(X3)
+        mask_negated(LAST_PIECE)
+        subtract_on_tensor(LAST_PIECE)
+        high_from_negated(LAST_PIECE)
+        for t in CHUNKS[0]:
+            truncate(w_span(t))
+        round_turned(LAST_PIECE)
         quantize_x(0, 2, HI)
         mask(x_span(2))
         quantize_x(0, 2, LO)
         subtract(x_span(2))
         quantize_x(2, 2, HI)
-        mask_negated(2)
-        subtract_on_tensor(2)
-        turn_back(X3)
-        truncate(w_span(3))
-        truncate(w_span(4))
-        low_from_back(X3)
-        mask(w_span(0))
-        mask(w_span(1))
-        subtract(w_span(0))
-        quantize_slots(0, HI, 2)
-        multiply_pair(0, [(HI, HI)])
-        subtract(w_span(1))
-        round_turned(2)
-        prepare(5)
-        high_from_negated(2)
-        mask(w_span(3, 2))
-        quantize_slots(0, LO, 2)
-        multiply_pair(0, [(LO, HI)])
+        mask_negated(EARLY_TILE)
+        subtract_on_tensor(EARLY_TILE)
+        turn_back(LAST_PIECE)
+        for t in CHUNKS[1]:
+            truncate(w_span(t))
+        low_from_back(LAST_PIECE)
+
+        for t in CHUNKS[0]:
+            mask(w_span(t))
+        subtract(w_span(CHUNKS[0][0]))
+        quantize_chunk(0, (HI,))
+        multiply(0, [(HI, HI)])
+        subtract(w_span(CHUNKS[0][1]))
+        round_turned(EARLY_TILE)
+        prepare(GPSIMD_TILE[2])
+        high_from_negated(EARLY_TILE)
+
+        mask(w_span(CHUNKS[1][0], 2))
+        quantize_chunk(0, (LO,))
+        multiply(0, [(LO, HI)])
         quantize_x(2, 2, LO)
-        multiply_pair(0, [(HI, LO)])
-        subtract(w_span(3))
-        subtract(w_span(4))
-        prepare(6, 2)
-        mask_negated(9)
-        turn_back(2)
-        subtract_on_tensor(9)
-        low_from_back(2)
-        round_turned(9)
-        prepare(8)
-        mask(w_span(5))
-        subtract_on_gpsimd(5)
-        quantize_and_multiply(3)
-        read_out(0, 1)
-        mask_negated(11)
-        subtract_on_tensor(11)
-        high_from_negated(9)
-        round_turned(11)
-        prepare(10)
-        mask(w_span(6, 2))
-        subtract_on_gpsimd(6)
-        quantize_and_multiply(2)
-        read_out(3, 4)
-        subtract(w_span(7))
-        turn_back(9, 11)
-        low_from_back(9)
-        high_from_negated(11)
-        low_from_back(11)
-        mask(w_span(8))
-        subtract_on_gpsimd(8)
-        quantize_and_multiply(6)
-        read_out(2, 5)
-        mask(w_span(10))
-        subtract_on_gpsimd(10)
-        quantize_and_multiply(8)
-        read_out(6, 7)
-        quantize_slots(10, HI, 2)
-        quantize_slots(10, LO, 2)
-        multiply_pair(10, ALL_PRODUCTS)
-        read_out(8, 9, 10)
-        t = TILES - 1
-        stage = results[t][1]
+        multiply(0, [(HI, LO)])
+        for t in CHUNKS[1]:
+            subtract(w_span(t))
+        prepare(GPSIMD_TILE[3], 2)
+
+        mask_negated(MIDDLE_TILE)
+        turn_back(EARLY_TILE)
+        subtract_on_tensor(MIDDLE_TILE)
+        low_from_back(EARLY_TILE)
+        round_turned(MIDDLE_TILE)
+        prepare(GPSIMD_TILE[4])
+        step(2)
+
+        mask_negated(LAST_TILE)
+        subtract_on_tensor(LAST_TILE)
+        high_from_negated(MIDDLE_TILE)
+        round_turned(LAST_TILE)
+        prepare(GPSIMD_TILE[LAST])
+        step(3, 2)
+        subtract(w_span(VECTOR_TILE))
+
+        turn_back(MIDDLE_TILE, LAST_TILE)
+        low_from_back(MIDDLE_TILE)
+        high_from_negated(LAST_TILE)
+        low_from_back(LAST_TILE)
+        step(4)
+        step(LAST)
+
+        quantize_chunk(LAST, (HI,))
+        quantize_chunk(LAST, (LO,))
+        multiply(LAST, PRODUCTS)
+        read_out(*CHUNKS[LAST - 1], CHUNKS[LAST][0])
+        stage = results[LAST_TILE][1]
         for half in (slice(0, T // 2), slice(T // 2, T)):
-            nc.vector.tensor_tensor(out=stage[:, 0, half], in0=sums[t][:, half], in1=g_sb[t][:, half], op=ALU.mult)
-            nc.sync.dma_start(out=out_tiles[:, t, half], in_=stage[:, 0, half])
+            nc.vector.tensor_tensor(
+                out=stage[:, 0, half], in0=sums[LAST_TILE][:, half], in1=g_sb[LAST_TILE][:, half], op=ALU.mult
+            )
+            nc.sync.dma_start(out=out_tiles[:, LAST_TILE, half], in_=stage[:, 0, half])

@@ -21,7 +21,7 @@ HI, LO = 0, 1
 MX_ALIGN = 64
 DMA_ALIGN = 2048
 
-SUM_BANKS, TURNED_BANKS, BACK_BANKS = 5, 2, 1
+SUM_BANKS, TURN_BANKS = 5, 3
 
 WORD_MASK = 0xFFF00000 - (1 << 32)
 PAIR_MASK = 0xFFF0FFF0 - (1 << 32)
@@ -31,18 +31,27 @@ PAIR_RUN, LINE_RUN = 2, 4
 ROWS_IN_RUNS = "p j (c i) -> p c j i"
 SIDE_BY_SIDE_IN_RUNS = "p (c i j) -> p c j i"
 
-CHUNKS = [(0, 1), (3, 4), (2, 5), (6, 7), (8, 9), (10, 11)]
+CHUNKS = [(0, 1), (2, 3), (4, 5), (6, 7), (8, 9), (10, 11)]
 LAST = len(CHUNKS) - 1
 GPSIMD_TILE = {2: 5, 3: 6, 4: 8, 5: 10}
 LAST_PIECE = "last piece of x"
-EARLY_TILE, MIDDLE_TILE, LAST_TILE = 2, 9, 11
+EARLY_TILE, MIDDLE_TILE, LAST_TILE = 4, 9, 11
 VECTOR_TILE = 7
 
 LOADS = [
-    ("x", range(0, 1)), ("x", range(1, 2)), ("x", range(2, 4)), ("w", range(0, 2)), ("w", range(2, 4)), ("w", range(4, 6)),
-    ("w", range(6, 10)), ("g", range(0, 2)), ("w", range(10, 12)), ("g", range(3, 5)), ("g", range(2, 6, 3)), ("g", range(6, 12)),
+    ("x", range(0, 1)), ("x", range(1, 2)), ("x", range(2, 4)), ("w", range(0, 2)), ("w", range(4, 6)), ("w", range(2, 4)),
+    ("w", range(6, 10)), ("g", range(0, 2)), ("w", range(10, 12)), ("g", range(2, 4)), ("g", range(4, 8)), ("g", range(8, 12)),
 ]
-STORES = [range(0, 2), range(3, 5), range(2, 6, 3), range(6, 8)] + [range(t, t + 1) for t in range(8, 12)]
+STORES = [range(0, 4), range(5, 7)] + [range(t, t + 1) for t in (4, 7, 8, 9, 10, 11)]
+
+CALLS = [
+    [(0, HI), (1, HI)], [(0, LO), (1, LO)],
+    [(2, HI), (3, HI), (2, LO), (3, LO)],
+    [(5, HI), (6, HI), (5, LO), (6, LO)],
+    [(4, HI), (4, LO)], [(7, HI), (7, LO), (8, HI), (8, LO)],
+    [(10, HI)], [(10, LO), (9, HI), (9, LO), (11, HI)],
+    [(11, LO)],
+]
 
 PRODUCTS = [(HI, HI), (HI, LO), (LO, HI)]
 
@@ -52,8 +61,7 @@ def tile_mix_split3_fm_mul_kernel(tc, w, x, g, out):
     with ExitStack() as ctx:
         sb = ctx.enter_context(tc.tile_pool(name="sb", bufs=1))
         psum_sums = ctx.enter_context(tc.psum_pool(name="psum_sums", bufs=SUM_BANKS))
-        psum_turned = ctx.enter_context(tc.psum_pool(name="psum_turned", bufs=TURNED_BANKS))
-        psum_back = ctx.enter_context(tc.psum_pool(name="psum_back", bufs=BACK_BANKS))
+        psum_turns = ctx.enter_context(tc.psum_pool(name="psum_turns", bufs=TURN_BANKS))
         ctx.enter_context(tc.manual_schedule())
 
         k_rows = {"x": x.rearrange("(p j) t -> p j t", j=PACK), "w": w.rearrange("(p j) n -> p j n", j=PACK)}
@@ -86,25 +94,25 @@ def tile_mix_split3_fm_mul_kernel(tc, w, x, g, out):
         x_parts = [sb.tile([P, T * PACK], BF16, name=f"x_parts{h}", align_bytes=MX_ALIGN) for h in (HI, LO)]
         x_codes = sb.tile([P, 2, T], U32, name="x_codes", align_bytes=MX_ALIGN)
         x_scales = sb.tile([P, 2, T], U8, name="x_scales", align_bytes=MX_ALIGN)
-        w_parts, w_codes, w_scales, slots = {}, {}, {}, {}
-        for tiles in CHUNKS:
-            count = 2 * len(tiles)
-            parts = sb.tile([P, count * slot_size], BF16, name=f"w_parts{tiles[0]}", align_bytes=MX_ALIGN)
-            codes = sb.tile([P, count * P], U32, name=f"w_codes{tiles[0]}", align_bytes=MX_ALIGN)
-            scales = sb.tile([P, count * P], U8, name=f"w_scales{tiles[0]}", align_bytes=MX_ALIGN)
-            for a, t in enumerate(tiles):
-                w_parts[t], w_codes[t], w_scales[t] = parts, codes, scales
-                for h in (HI, LO):
-                    slots[t, h] = h * len(tiles) + a
+        w_parts, w_codes, w_scales, slots = [], [], [], {}
+        for call, members in enumerate(CALLS):
+            count = len(members)
+            if members == [(11, LO)]:
+                w_parts.append(w_parts[slots[10, HI][0]])
+            else:
+                w_parts.append(sb.tile([P, count * slot_size], BF16, name=f"w_parts{call}", align_bytes=MX_ALIGN))
+            w_codes.append(sb.tile([P, count * P], U32, name=f"w_codes{call}", align_bytes=MX_ALIGN))
+            w_scales.append(sb.tile([P, count * P], U8, name=f"w_scales{call}", align_bytes=MX_ALIGN))
+            for a, member in enumerate(members):
+                slots[member] = (call, a)
 
         def x_span(i):
             cols = slice(i * slot_size, (i + 1) * slot_size)
             return place["x", i] + (P, x_parts[HI][:, cols], x_parts[LO][:, cols])
 
         def w_span(t, count=1):
-            high, low = slots[t, HI] * slot_size, slots[t, LO] * slot_size
-            size = count * slot_size
-            return place["w", t] + (count * P, w_parts[t][:, high : high + size], w_parts[t][:, low : low + size])
+            parts = [w_parts[call][:, a * slot_size : (a + count) * slot_size] for call, a in (slots[t, HI], slots[t, LO])]
+            return place["w", t] + (count * P, parts[HI], parts[LO])
 
         def span_of(t):
             return x_span(T // P - 1) if t == LAST_PIECE else w_span(t)
@@ -133,13 +141,11 @@ def tile_mix_split3_fm_mul_kernel(tc, w, x, g, out):
         laid_out = {}
 
         def prepare(t, count=1):
-            laid_out[t] = sb.tile([P, slot_size], F32, name=f"laid_out{t}", align_bytes=MX_ALIGN)
-            nc.scalar.copy(out=in_runs(laid_out[t][:]), in_=rows_in_runs(raw(w_span(t))))
             truncate(w_span(t, count))
 
         def subtract_on_gpsimd(t):
-            high, low = w_span(t)[3:]
-            nc.gpsimd.tensor_tensor(out=low, in0=laid_out[t][:], in1=high, op=ALU.subtract)
+            span = w_span(t)
+            nc.gpsimd.tensor_tensor(out=in_runs(span[4]), in0=rows_in_runs(raw(span)), in1=in_runs(span[3]), op=ALU.subtract)
 
         negated = {}
         turned = {}
@@ -157,8 +163,12 @@ def tile_mix_split3_fm_mul_kernel(tc, w, x, g, out):
                 op1=ALU.bitwise_xor,
             )
 
+        def negated_from_high(t):
+            negated[t] = sb.tile([P, PACK, P], F32, name=f"negated{len(negated)}", align_bytes=MX_ALIGN)
+            nc.scalar.activation(out=rows_in_runs(negated[t][:], LINE_RUN), in_=in_runs(span_of(t)[3], LINE_RUN), func=ACT.Copy, scale=-1.0)
+
         def subtract_on_tensor(t):
-            turned[t] = psum_turned.tile([P, PACK, P], F32, name="turned")
+            turned[t] = psum_turns.tile([P, PACK, P], F32, name="turns")
             terms = [raw(span_of(t)), negated[t][:]]
             for s, rows in enumerate(terms):
                 for j in range(PACK):
@@ -179,7 +189,7 @@ def tile_mix_split3_fm_mul_kernel(tc, w, x, g, out):
             )
 
         def turn_back(*tiles):
-            bank = psum_back.tile([P, 2, 2, P], F32, name="back")
+            bank = psum_turns.tile([P, 2, 2, P], F32, name="turns")
             for a, t in enumerate(tiles):
                 words = rounded[t][:].bitcast(F32)
                 for u in range(2):
@@ -201,32 +211,33 @@ def tile_mix_split3_fm_mul_kernel(tc, w, x, g, out):
                 out=x_codes[:, h, t0:t1].bitcast(FP8X4), scales=x_scales[:, h, t0:t1], in_=x_parts[h][:, t0 * PACK : t1 * PACK]
             )
 
-        def quantize_chunk(c, parts):
-            t = CHUNKS[c][0]
-            n0, n1 = slots[t, parts[0]] * P, (slots[t, parts[-1]] + len(CHUNKS[c])) * P
-            nc.vector.quantize_mx(
-                out=w_codes[t][:, n0:n1].bitcast(FP8X4), scales=w_scales[t][:, n0:n1], in_=w_parts[t][:, n0 * PACK : n1 * PACK]
-            )
+        def quantize_w(call):
+            nc.vector.quantize_mx(out=w_codes[call][:].bitcast(FP8X4), scales=w_scales[call][:], in_=w_parts[call][:])
 
         sums = {}
         passes = {}
 
-        def multiply(c, products):
-            for t in CHUNKS[c]:
-                for w_part, x_part in products:
-                    passes[t] = passes.get(t, 0) + 1
-                    if passes[t] == 1:
-                        sums[t] = psum_sums.tile([P, T], F32, name="sums")
-                    cols = slice(slots[t, w_part] * P, (slots[t, w_part] + 1) * P)
-                    nc.tensor.matmul_mx(
-                        out=sums[t][:],
-                        lhsT=w_codes[t][:, cols].bitcast(FP8X4),
-                        lhsT_scale=w_scales[t][:, cols],
-                        rhs=x_codes[:, x_part, :].bitcast(FP8X4),
-                        rhs_scale=x_scales[:, x_part, :],
-                        start=passes[t] == 1,
-                        stop=passes[t] == len(PRODUCTS),
-                    )
+        def multiply(t, *products):
+            for w_part, x_part in products:
+                passes[t] = passes.get(t, 0) + 1
+                if passes[t] == 1:
+                    sums[t] = psum_sums.tile([P, T], F32, name="sums")
+                call, a = slots[t, w_part]
+                cols = slice(a * P, (a + 1) * P)
+                nc.tensor.matmul_mx(
+                    out=sums[t][:],
+                    lhsT=w_codes[call][:, cols].bitcast(FP8X4),
+                    lhsT_scale=w_scales[call][:, cols],
+                    rhs=x_codes[:, x_part, :].bitcast(FP8X4),
+                    rhs_scale=x_scales[:, x_part, :],
+                    start=passes[t] == 1,
+                    stop=passes[t] == len(PRODUCTS),
+                )
+
+        def quantize_and_multiply(call):
+            quantize_w(call)
+            for t in sorted({t for t, h in CALLS[call]}):
+                multiply(t, *[product for product in PRODUCTS if (t, product[0]) in CALLS[call]])
 
         read = set()
 
@@ -238,12 +249,11 @@ def tile_mix_split3_fm_mul_kernel(tc, w, x, g, out):
                 if all(u in read for u in together):
                     nc.sync.dma_start(out=out_tiles[:, together.start : together[-1] + 1 : together.step, :], in_=stage[:])
 
-        def step(c, masked=1):
-            mask(w_span(GPSIMD_TILE[c], masked))
-            subtract_on_gpsimd(GPSIMD_TILE[c])
-            quantize_chunk(c - 1, (HI, LO))
-            multiply(c - 1, PRODUCTS)
-            read_out(*CHUNKS[c - 2])
+        def release_gpsimd(t, call, *tiles, masked=1):
+            mask(w_span(t, masked))
+            subtract_on_gpsimd(t)
+            quantize_and_multiply(call)
+            read_out(*tiles)
 
         word_highs = []
         for i in range(2):
@@ -270,62 +280,71 @@ def tile_mix_split3_fm_mul_kernel(tc, w, x, g, out):
         quantize_x(0, 2, LO)
         subtract(x_span(2))
         quantize_x(2, 2, HI)
+        mask(w_span(0))
         mask_negated(EARLY_TILE)
         subtract_on_tensor(EARLY_TILE)
         turn_back(LAST_PIECE)
-        for t in CHUNKS[1]:
-            truncate(w_span(t))
+        truncate(w_span(2))
+        truncate(w_span(3))
         low_from_back(LAST_PIECE)
 
-        for t in CHUNKS[0]:
-            mask(w_span(t))
-        subtract(w_span(CHUNKS[0][0]))
-        quantize_chunk(0, (HI,))
-        multiply(0, [(HI, HI)])
-        subtract(w_span(CHUNKS[0][1]))
-        round_turned(EARLY_TILE)
-        prepare(GPSIMD_TILE[2])
-        high_from_negated(EARLY_TILE)
+        mask(w_span(1))
+        subtract(w_span(0))
+        quantize_w(0)
+        multiply(0, (HI, HI))
+        multiply(1, (HI, HI))
+        subtract(w_span(1))
+        truncate(w_span(5))
+        round_turned(4)
+        truncate(w_span(6))
+        high_from_negated(4)
+        truncate(w_span(7))
 
-        mask(w_span(CHUNKS[1][0], 2))
-        quantize_chunk(0, (LO,))
-        multiply(0, [(LO, HI)])
+        mask(w_span(2))
+        quantize_and_multiply(1)
+        mask(w_span(3))
+        subtract(w_span(2))
         quantize_x(2, 2, LO)
-        multiply(0, [(HI, LO)])
-        for t in CHUNKS[1]:
-            subtract(w_span(t))
-        prepare(GPSIMD_TILE[3], 2)
+        multiply(0, (HI, LO))
+        multiply(1, (HI, LO))
+        mask_negated(8)
+        subtract(w_span(3))
+        mask_negated(9)
+        subtract_on_tensor(8)
+        subtract_on_tensor(9)
+        mask(w_span(6))
+        round_turned(8)
+        truncate(w_span(11))
+        round_turned(9)
+        release_gpsimd(5, 2, 0, 1)
 
-        mask_negated(MIDDLE_TILE)
-        turn_back(EARLY_TILE)
-        subtract_on_tensor(MIDDLE_TILE)
-        low_from_back(EARLY_TILE)
-        round_turned(MIDDLE_TILE)
-        prepare(GPSIMD_TILE[4])
-        step(2)
+        subtract(w_span(6))
+        mask(w_span(11))
+        turn_back(4)
+        turn_back(8, 9)
+        high_from_negated(8)
+        truncate(w_span(10))
+        low_from_back(4)
+        low_from_back(8)
+        high_from_negated(9)
+        low_from_back(9)
+        release_gpsimd(7, 3, 2, 3)
 
-        mask_negated(LAST_TILE)
-        subtract_on_tensor(LAST_TILE)
-        high_from_negated(MIDDLE_TILE)
-        round_turned(LAST_TILE)
-        prepare(GPSIMD_TILE[LAST])
-        step(3, 2)
-        subtract(w_span(VECTOR_TILE))
+        quantize_and_multiply(4)
+        release_gpsimd(10, 5, 5, 6, 4)
 
-        turn_back(MIDDLE_TILE, LAST_TILE)
-        low_from_back(MIDDLE_TILE)
-        high_from_negated(LAST_TILE)
-        low_from_back(LAST_TILE)
-        step(4)
-        step(LAST)
+        quantize_and_multiply(6)
+        subtract_on_gpsimd(11)
+        quantize_w(7)
+        multiply(10, (LO, HI))
+        multiply(9, *PRODUCTS)
+        read_out(7)
+        multiply(11, (HI, HI), (HI, LO))
+        read_out(8, 10)
 
-        quantize_chunk(LAST, (HI,))
-        quantize_chunk(LAST, (LO,))
-        multiply(LAST, PRODUCTS)
-        read_out(*CHUNKS[LAST - 1], CHUNKS[LAST][0])
-        stage = results[LAST_TILE][1]
+        quantize_and_multiply(8)
+        read_out(9)
+        stage = results[11][1]
         for half in (slice(0, T // 2), slice(T // 2, T)):
-            nc.vector.tensor_tensor(
-                out=stage[:, 0, half], in0=sums[LAST_TILE][:, half], in1=g_sb[LAST_TILE][:, half], op=ALU.mult
-            )
-            nc.sync.dma_start(out=out_tiles[:, LAST_TILE, half], in_=stage[:, 0, half])
+            nc.vector.tensor_tensor(out=stage[:, 0, half], in0=sums[11][:, half], in1=g_sb[11][:, half], op=ALU.mult)
+            nc.sync.dma_start(out=out_tiles[:, 11, half], in_=stage[:, 0, half])

from contextlib import ExitStack

import concourse.mybir as mybir
from concourse.masks import make_identity

K, M, T = 512, 1536, 512
FLOPS = 3 * 2 * K * M * T

F32 = mybir.dt.float32
BF16 = mybir.dt.bfloat16
I32 = mybir.dt.int32
U32 = mybir.dt.uint32
U8 = mybir.dt.uint8
FP8X4 = mybir.dt.float8_e4m3fn_x4
ALU = mybir.AluOpType
ACT = mybir.ActivationFunctionType

P = 128
PACK = 4
HI, LO = 0, 1
MX_ALIGN = 64
DMA_ALIGN = 2048

SUM_BANKS, TURN_BANKS = 5, 3

WORD_MASK = 0xFFF00000 - (1 << 32)
PAIR_MASK = 0xFFF0FFF0 - (1 << 32)
SIGN_BIT = -(1 << 31)

PAIR_RUN, LINE_RUN = 2, 4
ROWS_IN_RUNS = "p j (c i) -> p c j i"
SIDE_BY_SIDE_IN_RUNS = "p (c i j) -> p c j i"

CHUNKS = [(0, 1), (2, 3), (4, 5), (6, 7), (8, 9), (10, 11)]
LAST = len(CHUNKS) - 1
GPSIMD_TILE = {2: 5, 3: 6, 4: 8, 5: 10}
LAST_PIECE = "last piece of x"
EARLY_TILE, MIDDLE_TILE, LAST_TILE = 4, 9, 11
VECTOR_TILE = 7

LOADS = [
    ("x", range(0, 1)), ("x", range(1, 2)), ("x", range(2, 4)), ("w", range(0, 2)), ("w", range(4, 6)), ("w", range(2, 4)),
    ("w", range(6, 10)), ("g", range(0, 2)), ("w", range(10, 12)), ("g", range(2, 4)), ("g", range(4, 8)), ("g", range(8, 12)),
]
STORES = [range(0, 4), range(5, 7)] + [range(t, t + 1) for t in (4, 7, 8, 9, 10, 11)]

CALLS = [
    [(0, HI), (1, HI)], [(0, LO), (1, LO)],
    [(2, HI), (3, HI), (2, LO), (3, LO)],
    [(5, HI), (6, HI), (5, LO), (6, LO)],
    [(4, HI), (4, LO)], [(7, HI), (7, LO), (8, HI), (8, LO)],
    [(10, HI)], [(10, LO), (9, HI), (9, LO), (11, HI)],
    [(11, LO)],
]

PRODUCTS = [(HI, HI), (HI, LO), (LO, HI)]


def tile_mix_split3_fm_mul_kernel(tc, w, x, g, out):
    nc = tc.nc
    with ExitStack() as ctx:
        sb = ctx.enter_context(tc.tile_pool(name="sb", bufs=1))
        psum_sums = ctx.enter_context(tc.psum_pool(name="psum_sums", bufs=SUM_BANKS))
        psum_turns = ctx.enter_context(tc.psum_pool(name="psum_turns", bufs=TURN_BANKS))
        ctx.enter_context(tc.manual_schedule())

        k_rows = {"x": x.rearrange("(p j) t -> p j t", j=PACK), "w": w.rearrange("(p j) n -> p j n", j=PACK)}
        g_tiles = g.rearrange("(a p) t -> p a t", p=P)
        out_tiles = out.rearrange("(a p) t -> p a t", p=P)
        place = {}
        g_sb = {}
        for operand, tiles in LOADS:
            first, count = tiles.start, len(tiles)
            if operand == "g":
                stage = sb.tile([P, count, T], F32, name=f"g_sb{first}", align_bytes=DMA_ALIGN)
                nc.sync.dma_start(out=stage[:], in_=g_tiles[:, first : tiles[-1] + 1 : tiles.step, :])
                for a, t in enumerate(tiles):
                    g_sb[t] = stage[:, a, :]
            else:
                stage = sb.tile([P, PACK, count * P], F32, name=f"{operand}_raw{first}", align_bytes=DMA_ALIGN)
                nc.sync.dma_start(out=stage[:], in_=k_rows[operand][:, :, first * P : (first + count) * P])
                for a in range(count):
                    place[operand, first + a] = (stage, a * P)
        results = {}
        for tiles in STORES:
            stage = sb.tile([P, len(tiles), T], F32, name=f"result{tiles.start}", align_bytes=DMA_ALIGN)
            for t in tiles:
                results[t] = (tiles, stage)

        identity = sb.tile([P, P], F32, name="identity", align_bytes=MX_ALIGN)
        make_identity(nc, identity[:])

        slot_size = P * PACK
        x_parts = [sb.tile([P, T * PACK], BF16, name=f"x_parts{h}", align_bytes=MX_ALIGN) for h in (HI, LO)]
        x_codes = sb.tile([P, 2, T], U32, name="x_codes", align_bytes=MX_ALIGN)
        x_scales = sb.tile([P, 2, T], U8, name="x_scales", align_bytes=MX_ALIGN)
        w_parts, w_codes, w_scales, slots = [], [], [], {}
        for call, members in enumerate(CALLS):
            count = len(members)
            if members == [(11, LO)]:
                w_parts.append(w_parts[slots[10, HI][0]])
            else:
                w_parts.append(sb.tile([P, count * slot_size], BF16, name=f"w_parts{call}", align_bytes=MX_ALIGN))
            w_codes.append(sb.tile([P, count * P], U32, name=f"w_codes{call}", align_bytes=MX_ALIGN))
            w_scales.append(sb.tile([P, count * P], U8, name=f"w_scales{call}", align_bytes=MX_ALIGN))
            for a, member in enumerate(members):
                slots[member] = (call, a)

        def x_span(i):
            cols = slice(i * slot_size, (i + 1) * slot_size)
            return place["x", i] + (P, x_parts[HI][:, cols], x_parts[LO][:, cols])

        def w_span(t, count=1):
            parts = [w_parts[call][:, a * slot_size : (a + count) * slot_size] for call, a in (slots[t, HI], slots[t, LO])]
            return place["w", t] + (count * P, parts[HI], parts[LO])

        def span_of(t):
            return x_span(T // P - 1) if t == LAST_PIECE else w_span(t)

        def raw(span):
            return span[0][:, :, span[1] : span[1] + span[2]]

        def rows_in_runs(rows, run=PAIR_RUN):
            return rows.rearrange(ROWS_IN_RUNS, i=run)

        def in_runs(part, run=PAIR_RUN):
            return part.rearrange(SIDE_BY_SIDE_IN_RUNS, i=run, j=PACK)

        def truncate(span):
            stage, first, width, high = span[:4]
            halves = stage[:].bitcast(BF16).rearrange("p j (c i h) -> p c j i h", i=LINE_RUN, h=2)
            nc.scalar.copy(out=in_runs(high, LINE_RUN), in_=halves[:, first // LINE_RUN : (first + width) // LINE_RUN, :, :, 1])

        def mask(span):
            words = span[3].bitcast(I32)
            nc.vector.tensor_scalar(out=words, in0=words, scalar1=PAIR_MASK, scalar2=None, op0=ALU.bitwise_and)

        def subtract(span):
            nc.vector.tensor_tensor(out=in_runs(span[4]), in0=rows_in_runs(raw(span)), in1=in_runs(span[3]), op=ALU.subtract)

        laid_out = {}

        def prepare(t, count=1):
            truncate(w_span(t, count))

        def subtract_on_gpsimd(t):
            span = w_span(t)
            nc.gpsimd.tensor_tensor(out=in_runs(span[4]), in0=rows_in_runs(raw(span)), in1=in_runs(span[3]), op=ALU.subtract)

        negated = {}
        turned = {}
        rounded = {}
        back = {}

        def mask_negated(t):
            negated[t] = sb.tile([P, PACK, P], F32, name=f"negated{len(negated)}", align_bytes=MX_ALIGN)
            nc.vector.tensor_scalar(
                out=negated[t][:].bitcast(I32),
                in0=raw(span_of(t)).bitcast(I32),
                scalar1=WORD_MASK,
                scalar2=SIGN_BIT,
                op0=ALU.bitwise_and,
                op1=ALU.bitwise_xor,
            )

        def negated_from_high(t):
            negated[t] = sb.tile([P, PACK, P], F32, name=f"negated{len(negated)}", align_bytes=MX_ALIGN)
            nc.scalar.activation(out=rows_in_runs(negated[t][:], LINE_RUN), in_=in_runs(span_of(t)[3], LINE_RUN), func=ACT.Copy, scale=-1.0)

        def subtract_on_tensor(t):
            turned[t] = psum_turns.tile([P, PACK, P], F32, name="turns")
            terms = [raw(span_of(t)), negated[t][:]]
            for s, rows in enumerate(terms):
                for j in range(PACK):
                    nc.tensor.matmul(
                        turned[t][:, j, :],
                        lhsT=rows[:, j, :],
                        rhs=identity[:],
                        is_transpose=True,
                        start=s == 0 and j == 0,
                        stop=s == len(terms) - 1 and j == PACK - 1,
                    )

        def round_turned(t):
            rounded[t] = sb.tile([P, slot_size], BF16, name=f"rounded{len(rounded)}", align_bytes=MX_ALIGN)
            nc.scalar.copy(
                out=rounded[t][:].rearrange("n (u p e) -> n u p e", u=2, e=2),
                in_=turned[t][:].rearrange("n (u e) p -> n u p e", e=2),
            )

        def turn_back(*tiles):
            bank = psum_turns.tile([P, 2, 2, P], F32, name="turns")
            for a, t in enumerate(tiles):
                words = rounded[t][:].bitcast(F32)
                for u in range(2):
                    nc.tensor.transpose(bank[:, a, u, :], words[:, u * P : (u + 1) * P], identity[:])
                back[t] = bank[:, a, :, :]

        def low_from_back(t):
            nc.scalar.copy(
                out=span_of(t)[4].bitcast(F32).rearrange("p (n u) -> p n u", u=2),
                in_=back[t].rearrange("p u n -> p n u"),
            )

        def high_from_negated(t):
            nc.scalar.activation(out=in_runs(span_of(t)[3], LINE_RUN), in_=rows_in_runs(negated[t][:], LINE_RUN), func=ACT.Copy, scale=-1.0)

        def quantize_x(first, count, h):
            t0, t1 = first * P, (first + count) * P
            nc.vector.quantize_mx(
                out=x_codes[:, h, t0:t1].bitcast(FP8X4), scales=x_scales[:, h, t0:t1], in_=x_parts[h][:, t0 * PACK : t1 * PACK]
            )

        def quantize_w(call):
            nc.vector.quantize_mx(out=w_codes[call][:].bitcast(FP8X4), scales=w_scales[call][:], in_=w_parts[call][:])

        sums = {}
        passes = {}

        def multiply(t, *products):
            for w_part, x_part in products:
                passes[t] = passes.get(t, 0) + 1
                if passes[t] == 1:
                    sums[t] = psum_sums.tile([P, T], F32, name="sums")
                call, a = slots[t, w_part]
                cols = slice(a * P, (a + 1) * P)
                nc.tensor.matmul_mx(
                    out=sums[t][:],
                    lhsT=w_codes[call][:, cols].bitcast(FP8X4),
                    lhsT_scale=w_scales[call][:, cols],
                    rhs=x_codes[:, x_part, :].bitcast(FP8X4),
                    rhs_scale=x_scales[:, x_part, :],
                    start=passes[t] == 1,
                    stop=passes[t] == len(PRODUCTS),
                )

        def quantize_and_multiply(call):
            quantize_w(call)
            for t in sorted({t for t, h in CALLS[call]}):
                multiply(t, *[product for product in PRODUCTS if (t, product[0]) in CALLS[call]])

        read = set()

        def read_out(*tiles):
            for t in tiles:
                together, stage = results[t]
                nc.vector.tensor_tensor(out=stage[:, together.index(t), :], in0=sums[t][:], in1=g_sb[t], op=ALU.mult)
                read.add(t)
                if all(u in read for u in together):
                    nc.sync.dma_start(out=out_tiles[:, together.start : together[-1] + 1 : together.step, :], in_=stage[:])

        def release_gpsimd(t, call, *tiles, masked=1):
            mask(w_span(t, masked))
            subtract_on_gpsimd(t)
            quantize_and_multiply(call)
            read_out(*tiles)

        word_highs = []
        for i in range(2):
            words = sb.tile([P, PACK, P], F32, name=f"word_high{i}", align_bytes=MX_ALIGN)
            nc.vector.tensor_scalar(
                out=words[:].bitcast(I32), in0=raw(x_span(i)).bitcast(I32), scalar1=WORD_MASK, scalar2=None, op0=ALU.bitwise_and
            )
            nc.scalar.copy(out=in_runs(x_span(i)[3], LINE_RUN), in_=rows_in_runs(words[:], LINE_RUN))
            word_highs.append(words)
        for i in range(2):
            nc.vector.tensor_tensor(
                out=in_runs(x_span(i)[4]), in0=rows_in_runs(raw(x_span(i))), in1=rows_in_runs(word_highs[i][:]), op=ALU.subtract
            )

        truncate(x_span(2))
        mask_negated(LAST_PIECE)
        subtract_on_tensor(LAST_PIECE)
        high_from_negated(LAST_PIECE)
        for t in CHUNKS[0]:
            truncate(w_span(t))
        round_turned(LAST_PIECE)
        quantize_x(0, 2, HI)
        mask(x_span(2))
        quantize_x(0, 2, LO)
        subtract(x_span(2))
        quantize_x(2, 2, HI)
        mask(w_span(0))
        mask_negated(EARLY_TILE)
        subtract_on_tensor(EARLY_TILE)
        turn_back(LAST_PIECE)
        truncate(w_span(2))
        truncate(w_span(3))
        low_from_back(LAST_PIECE)

        mask(w_span(1))
        subtract(w_span(0))
        quantize_w(0)
        multiply(0, (HI, HI))
        multiply(1, (HI, HI))
        subtract(w_span(1))
        truncate(w_span(5))
        round_turned(4)
        truncate(w_span(6))
        high_from_negated(4)
        truncate(w_span(7))

        mask(w_span(2))
        quantize_and_multiply(1)
        mask(w_span(3))
        subtract(w_span(2))
        quantize_x(2, 2, LO)
        multiply(0, (HI, LO))
        multiply(1, (HI, LO))
        mask_negated(8)
        subtract(w_span(3))
        mask_negated(9)
        subtract_on_tensor(8)
        subtract_on_tensor(9)
        mask(w_span(6))
        round_turned(8)
        truncate(w_span(11))
        round_turned(9)
        release_gpsimd(5, 2, 0, 1)

        subtract(w_span(6))
        mask(w_span(11))
        turn_back(4)
        turn_back(8, 9)
        high_from_negated(8)
        truncate(w_span(10))
        low_from_back(4)
        low_from_back(8)
        high_from_negated(9)
        low_from_back(9)
        release_gpsimd(7, 3, 2, 3)

        quantize_and_multiply(4)
        release_gpsimd(10, 5, 5, 6, 4)

        quantize_and_multiply(6)
        subtract_on_gpsimd(11)
        quantize_w(7)
        multiply(10, (LO, HI))
        multiply(9, *PRODUCTS)
        read_out(7)
        multiply(11, (HI, HI), (HI, LO))
        read_out(8, 10)

        quantize_and_multiply(8)
        read_out(9)
        stage = results[11][1]
        for half in (slice(0, T // 2), slice(T // 2, T)):
            nc.vector.tensor_tensor(out=stage[:, 0, half], in0=sums[11][:, half], in1=g_sb[11][:, half], op=ALU.mult)
            nc.sync.dma_start(out=out_tiles[:, 11, half], in_=stage[:, 0, half])
